import numpy as np
import ml_dtypes


def mxq(x, axis, fmt="e4m3"):
    dtype, down = {"e4m3": (ml_dtypes.float8_e4m3fn, 7), "e5m2": (ml_dtypes.float8_e5m2, 14)}[fmt]
    v = np.moveaxis(np.asarray(x, np.float32).astype(ml_dtypes.bfloat16).astype(np.float64), axis, -1)
    blocks = v.reshape(v.shape[:-1] + (-1, 32))
    amax = np.abs(blocks).max(-1, keepdims=True)
    byte = np.maximum(np.where(amax > 0, np.frexp(amax)[1] - 1 + 127, 0) - down, 1)
    scale = np.exp2(byte - 127.0)
    codes = (blocks / scale).astype(np.float32).astype(dtype).astype(np.float64)
    return np.moveaxis((codes * scale).reshape(v.shape), -1, axis)


WIDE = False


def mx_kscale(k):
    if not WIDE:
        return np.ones(k)
    levels = np.array([10, -10, 5, -5, 0])
    if k % 512:
        return np.exp2(np.random.permutation(np.resize(levels, k // 32))).repeat(32)
    a = np.empty((k // 512, 16))
    for p in range(k // 512):
        a[p, :8] = np.random.permutation(np.resize(levels, 8))
        for g in range(8):
            far = levels[np.abs(levels - a[p, g]) >= 10]
            a[p, g + 8] = far[np.random.randint(len(far))]
    return np.exp2(a.ravel()).repeat(32)


def f64(x):
    return np.asarray(x).astype(np.float64)


def striped(idx):
    return np.tile(idx.reshape(-1, 16).T, (8, 1)).astype(np.uint16)


def unstriped(offs):
    return offs[:16].T.reshape(-1).astype(np.int64)


E2M1 = np.array([0.0, 0.5, 1.0, 1.5, 2.0, 3.0, 4.0, 6.0, -0.0, -0.5, -1.0, -1.5, -2.0, -3.0, -4.0, -6.0])


def pack_weight(w, fmt):
    k, n = w.shape
    w = f64(np.asarray(w, np.float32).astype(ml_dtypes.bfloat16)).reshape(k // 32, 32, n)
    amax = np.abs(w).max(1)
    if fmt == "e4m3":
        byte = np.frexp(amax)[1] - 1 + 127 - 7
    else:
        mant, ex = np.frexp(amax / 6.0)
        byte = np.where(mant > 0.5, ex, ex - 1) + 127
    byte = np.clip(np.where(amax > 0, byte, 1), 1, 254)
    scaled = (w * np.exp2(127.0 - byte)[:, None, :]).reshape(k, n).astype(np.float32)
    by_word = np.ascontiguousarray(scaled.reshape(k // 512, 128, 4, n).transpose(0, 1, 3, 2))
    if fmt == "e4m3":
        words = by_word.astype(ml_dtypes.float8_e4m3fn).view(np.uint8)
    else:
        c = by_word.astype(ml_dtypes.float4_e2m1fn).view(np.uint8) & 0xF
        words = (c[..., 0::2] | (c[..., 1::2] << 4)).reshape(k // 512, 128, 2 * n)
    return np.ascontiguousarray(words), np.ascontiguousarray(byte.astype(np.uint8).reshape(k // 512, 16, n))


def unpack_weight(words, scales, fmt):
    g, _, n = scales.shape
    words = np.ascontiguousarray(words).reshape(g, 128, n, -1)
    if fmt == "e4m3":
        vals = words.view(ml_dtypes.float8_e4m3fn).astype(np.float64)
    else:
        nib = np.empty((g, 128, n, 4), np.uint8)
        nib[..., 0::2] = words & 0xF
        nib[..., 1::2] = words >> 4
        vals = E2M1[nib]
    vals = vals * np.repeat(np.exp2(scales.astype(np.float64) - 127.0), 8, axis=1)[..., None]
    return vals.transpose(0, 1, 3, 2).reshape(g * 512, n)


def gelu(v):
    return 0.5 * v * (1.0 + np.tanh(np.sqrt(2.0 / np.pi) * (v + 0.044715 * v**3)))


def pack_table4(v):
    words, scales = pack_weight(v, "e2m1")
    g, t = words.shape[0] // 2, v.shape[1]
    words = words.reshape(g, 2, 128, t, 2).transpose(0, 2, 3, 1, 4)
    return np.concatenate([words.reshape(g, -1), scales.reshape(g, -1)], axis=1)


def unpack_table4(tab):
    g, t = tab.shape[0], tab.shape[1] // 544
    words = tab[:, :512 * t].reshape(g, 128, t, 2, 2).transpose(0, 3, 1, 2, 4).reshape(2 * g, 128, 2 * t)
    return unpack_weight(words, tab[:, 512 * t:].reshape(2 * g, 16, t), "e2m1")


K, T, S, H, N = 1024, 4096, 1024, 1024, 512


def setup_inputs():
    n = np.random.standard_normal
    s = mx_kscale(K)[:, None]
    u = mx_kscale(H)[:, None]
    tab = pack_table4(n((K, T)) * s)
    wg_words, wg_scales = pack_weight(n((K, H)) / np.sqrt(K) / s, "e2m1")
    return {
        "tab": tab,
        "offs": striped(np.random.permutation(T)[:S]),
        "wv": (n((K, H)) / np.sqrt(K) / s * u.T).astype(np.float32),
        "wg_words": wg_words,
        "wg_scales": wg_scales,
        "bg": (0.5 * n(H)).astype(np.float32),
        "wo": (n((H, N)) / np.sqrt(H) / u).astype(np.float32),
        "bo": (0.3 * n(N)).astype(np.float32),
    }


def reference(tab, offs, wv, wg_words, wg_scales, bg, wo, bo):
    v = unpack_table4(tab)[:, unstriped(offs)]
    wgm = unpack_weight(wg_words, wg_scales, "e2m1")
    a = mxq(f64(wv), 0, "e4m3").T @ v
    z = (wgm.T @ v) + f64(bg)[:, None]
    g = 1.0 / (1.0 + np.exp(-z))
    h = a * g
    hq = mxq(h, 0, "e4m3")
    out = (mxq(f64(wo), 0, "e4m3").T @ hq) + f64(bo)[:, None]
    return out

@@ -1,0 +1,276 @@
+from contextlib import ExitStack
+
+import concourse.mybir as mybir
+from concourse.masks import make_identity
+
+K, T, S, H, N = 1024, 4096, 1024, 1024, 512
+FLOPS = 2 * (2 * K * H * S + H * N * S)
+
+F32 = mybir.dt.float32
+BF16 = mybir.dt.bfloat16
+I32 = mybir.dt.int32
+U32 = mybir.dt.uint32
+U16 = mybir.dt.uint16
+U8 = mybir.dt.uint8
+FP8X4 = mybir.dt.float8_e4m3fn_x4
+FP4X4 = mybir.dt.float4_e2m1fn_x4
+ACT = mybir.ActivationFunctionType
+ALU = mybir.AluOpType
+
+P = 128
+HALF = 512
+CH = 128
+PIECES = [(0, 512), (512, 256), (768, 128), (896, 128)]
+
+
+def tile_list_gated_click_interests_kernel(tc, tab, offs, wv, wg_words, wg_scales, bg, wo, bo, out):
+    nc = tc.nc
+    with ExitStack() as ctx:
+        keep = ctx.enter_context(tc.tile_pool(name="keep", bufs=1))
+        bank_wide = ctx.enter_context(tc.psum_pool(name="bank_wide", bufs=5))
+        bank_val = ctx.enter_context(tc.psum_pool(name="bank_val", bufs=3))
+
+        def sb(name, shape, dt, tag=None):
+            return keep.tile(shape, dt, name=name, tag=tag or name, align_bytes=64)
+
+        offsets = keep.tile([P, S // 16], U16, name="offsets")
+        nc.sync.dma_start(offsets[:], offs)
+
+        tab32 = tab.bitcast(I32)
+        tab_words = sb("tab_words", [P, T], I32, tag="slot_words")
+        nc.sync.dma_start(tab_words[:], tab32[0, 0 : P * T].rearrange("(p t) -> p t", p=P))
+
+        tab_scales = sb("tab_scales", [P, T // 4], I32, tag="slot_scales")
+        nc.vector.memset(tab_scales[:], 0)
+        scale_rows = tab32[0, P * T :].rearrange("(h q r t) -> r q h t", h=2, q=4, r=4)
+        for r in range(4):
+            nc.scalar.dma_start(tab_scales[r:P:16, :], scale_rows[r])
+
+        wg_raw = sb("wg_raw", [P, 2, 512], I32)
+        nc.sync.dma_start(wg_raw[:], wg_words.bitcast(I32).rearrange("a p w -> p a w"))
+        wgs_raw = sb("wgs_raw", [P, 2, 256], I32)
+        nc.vector.memset(wgs_raw[:], 0)
+        wgs32 = wg_scales.bitcast(I32)
+        for q in range(4):
+            nc.gpsimd.dma_start(wgs_raw[32 * q : 32 * q + 4, :, :], wgs32[:, 4 * q : 4 * q + 4, :].rearrange("a r w -> r a w"))
+
+        picked_scales1 = sb("picked_scales1", [P, S // 4], I32)
+        nc.vector.memset(picked_scales1[:], 0)
+
+        bias_rows = sb("bias_rows", [P, 2, P], F32)
+        nc.gpsimd.memset(bias_rows[:], 0.0)
+        nc.gpsimd.dma_start(
+            bias_rows[0:4].rearrange("t b (ph el) -> t (b ph) el", el=4),
+            bg.rearrange("(x t el) -> t x el", t=4, el=4),
+        )
+        nc.gpsimd.dma_start(bias_rows[4:8, 0, :], bo.rearrange("(c p) -> c p", p=P))
+        identity = sb("identity", [P, P], F32)
+        make_identity(nc, identity[:])
+        turned = bank_wide.tile([P, 2, P], F32, name="wide")
+        for b in range(2):
+            nc.tensor.transpose(turned[:, b, :], bias_rows[:, b, :], identity[:])
+        bias_cols = sb("bias_cols", [P, 2, 8], F32)
+        nc.scalar.copy(bias_cols[:], turned[:, :, 0:8])
+
+        wv_raw = {}
+
+        def load_wv(b, a, tag):
+            raw = sb(f"wv_raw{b}{a}", [P, 4, 512], F32, tag=tag)
+            nc.sync.dma_start(raw[:], wv[512 * a : 512 * (a + 1), 512 * b : 512 * (b + 1)].rearrange("(p j) c -> p j c", j=4))
+            wv_raw[b, a] = raw
+
+        load_wv(0, 0, "slot_a")
+
+        picked_scales0 = sb("picked_scales0", [P, S], U8)
+        nc.vector.tensor_copy(picked_scales0[:], tab_scales[:].bitcast(U8).indirect(offsets[:]))
+        nc.scalar.dma_start(picked_scales1[0:112, :], picked_scales0[:].bitcast(I32)[16:128, :])
+        tab_planes = [picked_scales0[:], picked_scales1[:].bitcast(U8)]
+
+        load_wv(0, 1, "slot_scales")
+
+        parted = []
+
+        def gather_words(jh):
+            picked = sb(f"picked{jh}", [P, HALF], U32, tag=f"slot_picked{jh}")
+            nc.vector.tensor_copy(picked[:], tab_words[:].bitcast(U32).indirect(offsets[:, 32 * jh : 32 * (jh + 1)]))
+            part = sb(f"parted{jh}", [P, 2, 2 * HALF], U8)
+            nc.vector.tensor_copy(part[:].bitcast(U16), picked[:].bitcast(U16).rearrange("p (j h) -> p h j", h=2))
+            parted.append(part)
+
+        wgs = sb("wgs", [P, 4, 4, 32], I32)
+        nc.vector.tensor_copy(wgs[:], wgs_raw[:].rearrange("p a (b ph t) -> p (a b) t ph", b=2, t=4))
+        wg_perm = []
+
+        def permute_wg(b):
+            perm = sb(f"wg_perm{b}", [P, 2, 4, 64], I32)
+            nc.vector.tensor_copy(
+                perm[:].rearrange("p a t (ph e) -> p a t ph e", e=2),
+                wg_raw[:, :, 256 * b : 256 * (b + 1)].rearrange("p a (ph t e) -> p a t ph e", t=4, e=2),
+            )
+            wg_perm.append(perm)
+
+        gather_words(0)
+        load_wv(1, 0, "slot_picked0")
+        permute_wg(0)
+        gather_words(1)
+        permute_wg(1)
+        load_wv(1, 1, "slot_words")
+
+        gate = {}
+
+        def gate_tile(b, jh, t):
+            if t == 0:
+                gate[b, jh] = sb(f"gate{b}{jh}", [P, 4, HALF], F32)
+            z = bank_wide.tile([P, HALF], F32, name="wide")
+            for a in range(2):
+                nc.tensor.matmul_mx(
+                    out=z[:],
+                    lhsT=wg_perm[b][:, a, t, :].bitcast(FP4X4),
+                    lhsT_scale=wgs[:, 2 * a + b, t, :].bitcast(U8),
+                    rhs=parted[jh][:, a, :].bitcast(FP4X4),
+                    rhs_scale=tab_planes[a][:, HALF * jh : HALF * (jh + 1)],
+                    start=(a == 0),
+                    stop=(a == 1),
+                )
+            nc.scalar.activation(gate[b, jh][:, t, :], z[:], ACT.Sigmoid, bias=bias_cols[:, b, t : t + 1])
+
+        wv_bf, wv_codes, wv_scales = {}, {}, {}
+
+        def round_wv(b, a, on_vector):
+            bf = sb(f"wv_bf{b}{a}", [P, 4, 512], BF16)
+            dst = bf[:].rearrange("p t (ph el j) -> p t ph j el", el=4, j=4)
+            src = wv_raw[b, a][:].rearrange("p j (ph t el) -> p t ph j el", t=4, el=4)
+            if on_vector:
+                nc.vector.tensor_copy(dst, src)
+            else:
+                for t in range(4):
+                    nc.scalar.copy(dst[:, t], src[:, t])
+            wv_bf[b, a] = bf
+
+        def quantise_wv(b, a):
+            wv_codes[b, a] = sb(f"wv_codes{b}{a}", [P, 512], U32)
+            wv_scales[b, a] = sb(f"wv_scales{b}{a}", [P, 512], U8)
+            nc.vector.quantize_mx(
+                out=wv_codes[b, a][:].bitcast(FP8X4),
+                scales=wv_scales[b, a][:],
+                in_=wv_bf[b, a][:].rearrange("p t c -> p (t c)"),
+            )
+
+        h_bf = {}
+        h_codes = [sb(f"h_codes{b}", [P, S], U32) for b in range(2)]
+        h_scales = [sb(f"h_scales{b}", [P, S], U8) for b in range(2)]
+
+        def value_chunk(b, jc):
+            jh, j0 = divmod(jc * CH, HALF)
+            val = bank_val.tile([P, 4, CH], F32, name="val")
+            for t in range(4):
+                for a in range(2):
+                    nc.tensor.matmul_mx(
+                        out=val[:, t, :],
+                        lhsT=wv_codes[b, a][:, P * t : P * (t + 1)].bitcast(FP8X4),
+                        lhsT_scale=wv_scales[b, a][:, P * t : P * (t + 1)],
+                        rhs=parted[jh][:, a, 2 * j0 : 2 * (j0 + CH)].bitcast(FP4X4),
+                        rhs_scale=tab_planes[a][:, jc * CH : (jc + 1) * CH],
+                        start=(a == 0),
+                        stop=(a == 1),
+                    )
+            h_bf[b, jc] = sb(f"h_bf{b}{jc}", [P, 4 * CH], BF16)
+            nc.vector.tensor_tensor(
+                h_bf[b, jc][:].rearrange("p (c i t) -> p c t i", i=4, t=4),
+                val[:].rearrange("p t (c i) -> p c t i", i=4),
+                gate[b, jh][:, :, j0 : j0 + CH].rearrange("p t (c i) -> p c t i", i=4),
+                ALU.mult,
+            )
+
+        def quantise_h(b, jc):
+            cols = slice(jc * CH, (jc + 1) * CH)
+            nc.vector.quantize_mx(out=h_codes[b][:, cols].bitcast(FP8X4), scales=h_scales[b][:, cols], in_=h_bf[b, jc][:])
+
+        wo_raw, wo_codes, wo_scales, wo_bf = {}, {}, {}, {}
+
+        def load_wo(b, tag):
+            raw = sb(f"wo_raw{b}", [P, 4, N], F32, tag=tag)
+            rows = wo[512 * b : 512 * (b + 1), :].rearrange("(ph t el) n -> t ph el n", t=4, el=4)
+            for t in range(4):
+                nc.sync.dma_start(raw[:, t, :], rows[t])
+            wo_raw[b] = raw
+
+        def round_wo(b, half):
+            if half == 0:
+                wo_bf[b] = sb(f"wo_bf{b}", [P, 4 * N], BF16)
+            nc.scalar.copy(
+                wo_bf[b][:, 1024 * half : 1024 * (half + 1)].rearrange("p (c i t) -> p c t i", i=4, t=4),
+                wo_raw[b][:, :, 256 * half : 256 * (half + 1)].rearrange("p t (c i) -> p c t i", i=4),
+            )
+
+        def quantise_wo(b):
+            wo_codes[b] = sb(f"wo_codes{b}", [P, N], U32)
+            wo_scales[b] = sb(f"wo_scales{b}", [P, N], U8)
+            nc.vector.quantize_mx(out=wo_codes[b][:].bitcast(FP8X4), scales=wo_scales[b][:], in_=wo_bf[b][:])
+
+        out_rows = out.rearrange("(nt p) j -> p nt j", p=P)
+
+        def out_piece(index):
+            j0, width = PIECES[index]
+            per_bank = 1 if width == 512 else 2
+            for nt0 in range(0, 4, per_bank):
+                acc = bank_wide.tile([P, per_bank, width], F32, name="wide")
+                res = sb(f"res{index}{nt0}", [P, per_bank, width], F32)
+                for i in range(per_bank):
+                    cols = slice(P * (nt0 + i), P * (nt0 + i + 1))
+                    for b in range(2):
+                        nc.tensor.matmul_mx(
+                            out=acc[:, i, :],
+                            lhsT=wo_codes[b][:, cols].bitcast(FP8X4),
+                            lhsT_scale=wo_scales[b][:, cols],
+                            rhs=h_codes[b][:, j0 : j0 + width].bitcast(FP8X4),
+                            rhs_scale=h_scales[b][:, j0 : j0 + width],
+                            start=(b == 0),
+                            stop=(b == 1),
+                        )
+                on_vector = index == len(PIECES) - 1 and nt0 == 0
+                for i in range(per_bank):
+                    bias = bias_cols[:, 0, 4 + nt0 + i : 5 + nt0 + i]
+                    if on_vector:
+                        nc.vector.tensor_scalar(res[:, i, :], acc[:, i, :], bias, None, ALU.add)
+                    else:
+                        nc.scalar.activation(res[:, i, :], acc[:, i, :], ACT.Identity, bias=bias)
+                nc.sync.dma_start(out_rows[:, nt0 : nt0 + per_bank, j0 : j0 + width], res[:])
+
+        for jh in range(2):
+            for t in range(4):
+                gate_tile(0, jh, t)
+        round_wv(0, 0, True)
+        quantise_wv(0, 0)
+        load_wo(0, "slot_a")
+        round_wv(0, 1, True)
+        quantise_wv(0, 1)
+        load_wo(1, "slot_scales")
+        for jc in range(8):
+            value_chunk(0, jc)
+            gate_tile(1, jc // 4, jc % 4)
+            if jc == 1:
+                round_wv(1, 0, False)
+            if jc == 2:
+                quantise_wv(1, 0)
+            if jc == 4:
+                round_wv(1, 1, False)
+            if jc == 5:
+                quantise_wv(1, 1)
+            if jc > 0:
+                quantise_h(0, jc - 1)
+        for b in range(2):
+            for half in range(2):
+                round_wo(b, half)
+        for jc in range(8):
+            value_chunk(1, jc)
+            quantise_h(*((0, 7) if jc == 0 else (1, jc - 1)))
+            if jc in (1, 2):
+                quantise_wo(jc - 1)
+            if jc == 4:
+                out_piece(0)
+            if jc == 6:
+                out_piece(1)
+        out_piece(2)
+        quantise_h(1, 7)
+        out_piece(3)

@@ -20,7 +20,7 @@ ALU = mybir.AluOpType
 P = 128
 HALF = 512
 CH = 128
-PIECES = [(0, 512), (512, 256), (768, 128), (896, 128)]
+PIECES = [(0, 256), (256, 256), (512, 256), (768, 128), (896, 128)]
 
 
 def tile_list_gated_click_interests_kernel(tc, tab, offs, wv, wg_words, wg_scales, bg, wo, bo, out):
@@ -37,18 +37,29 @@ def tile_list_gated_click_interests_kernel(tc, tab, offs, wv, wg_words, wg_scale
         nc.sync.dma_start(offsets[:], offs)
 
         tab32 = tab.bitcast(I32)
+        tab_scales = sb("tab_scales", [P, T // 4], I32, tag="slot_wg")
+        nc.vector.memset(tab_scales[:, 0:640], 0)
+        nc.gpsimd.memset(tab_scales[:, 640:1024], 0)
+        bias_rows = sb("bias_rows", [P, 2, P], F32)
+        nc.gpsimd.memset(bias_rows[:], 0.0)
+        nc.scalar.dma_start(
+            bias_rows[0:4].rearrange("t b (ph el) -> t (b ph) el", el=4),
+            bg.rearrange("(x t el) -> t x el", t=4, el=4),
+        )
+        identity = sb("identity", [P, P], F32)
+        make_identity(nc, identity[:])
+        warm = sb("warm", [P, 1], F32)
+        nc.scalar.activation(warm[:], identity[:, 0:1], ACT.Sigmoid)
+        wg_raw = sb("wg_raw", [P, 2, 512], I32)
+        for a in range(2):
+            nc.sync.dma_start(wg_raw[:, a, :], wg_words.bitcast(I32)[a])
+        scale_rows = tab32[0, P * T :].rearrange("(h q r t) -> r q h t", h=2, q=4, r=4)
+        for r in range(4):
+            nc.sync.dma_start(tab_scales[r:P:16, :], scale_rows[r])
         tab_words = sb("tab_words", [P, T], I32, tag="slot_words")
         nc.sync.dma_start(tab_words[:], tab32[0, 0 : P * T].rearrange("(p t) -> p t", p=P))
 
-        tab_scales = sb("tab_scales", [P, T // 4], I32, tag="slot_scales")
-        nc.vector.memset(tab_scales[:], 0)
-        scale_rows = tab32[0, P * T :].rearrange("(h q r t) -> r q h t", h=2, q=4, r=4)
-        for r in range(4):
-            nc.scalar.dma_start(tab_scales[r:P:16, :], scale_rows[r])
-
-        wg_raw = sb("wg_raw", [P, 2, 512], I32)
-        nc.sync.dma_start(wg_raw[:], wg_words.bitcast(I32).rearrange("a p w -> p a w"))
-        wgs_raw = sb("wgs_raw", [P, 2, 256], I32)
+        wgs_raw = sb("wgs_raw", [P, 2, 256], I32, tag="slot_wgs")
         nc.vector.memset(wgs_raw[:], 0)
         wgs32 = wg_scales.bitcast(I32)
         for q in range(4):
@@ -57,36 +68,24 @@ def tile_list_gated_click_interests_kernel(tc, tab, offs, wv, wg_words, wg_scale
         picked_scales1 = sb("picked_scales1", [P, S // 4], I32)
         nc.vector.memset(picked_scales1[:], 0)
 
-        bias_rows = sb("bias_rows", [P, 2, P], F32)
-        nc.gpsimd.memset(bias_rows[:], 0.0)
-        nc.gpsimd.dma_start(
-            bias_rows[0:4].rearrange("t b (ph el) -> t (b ph) el", el=4),
-            bg.rearrange("(x t el) -> t x el", t=4, el=4),
-        )
-        nc.gpsimd.dma_start(bias_rows[4:8, 0, :], bo.rearrange("(c p) -> c p", p=P))
-        identity = sb("identity", [P, P], F32)
-        make_identity(nc, identity[:])
         turned = bank_wide.tile([P, 2, P], F32, name="wide")
         for b in range(2):
             nc.tensor.transpose(turned[:, b, :], bias_rows[:, b, :], identity[:])
-        bias_cols = sb("bias_cols", [P, 2, 8], F32)
-        nc.scalar.copy(bias_cols[:], turned[:, :, 0:8])
+        bias_cols = sb("bias_cols", [P, 2, 4], F32)
+        nc.vector.tensor_copy(bias_cols[:], turned[:, :, 0:4])
 
         wv_raw = {}
 
-        def load_wv(b, a, tag):
-            raw = sb(f"wv_raw{b}{a}", [P, 4, 512], F32, tag=tag)
-            nc.sync.dma_start(raw[:], wv[512 * a : 512 * (a + 1), 512 * b : 512 * (b + 1)].rearrange("(p j) c -> p j c", j=4))
+        def load_wv(b, a, raw):
+            nc.sync.dma_start(raw, wv[512 * a : 512 * (a + 1), 512 * b : 512 * (b + 1)].rearrange("(p j) c -> p j c", j=4))
             wv_raw[b, a] = raw
 
-        load_wv(0, 0, "slot_a")
 
         picked_scales0 = sb("picked_scales0", [P, S], U8)
         nc.vector.tensor_copy(picked_scales0[:], tab_scales[:].bitcast(U8).indirect(offsets[:]))
-        nc.scalar.dma_start(picked_scales1[0:112, :], picked_scales0[:].bitcast(I32)[16:128, :])
+        nc.sync.dma_start(picked_scales1[0:112, :], picked_scales0[:].bitcast(I32)[16:128, :])
         tab_planes = [picked_scales0[:], picked_scales1[:].bitcast(U8)]
 
-        load_wv(0, 1, "slot_scales")
 
         parted = []
 
@@ -97,24 +96,30 @@ def tile_list_gated_click_interests_kernel(tc, tab, offs, wv, wg_words, wg_scale
             nc.vector.tensor_copy(part[:].bitcast(U16), picked[:].bitcast(U16).rearrange("p (j h) -> p h j", h=2))
             parted.append(part)
 
-        wgs = sb("wgs", [P, 4, 4, 32], I32)
-        nc.vector.tensor_copy(wgs[:], wgs_raw[:].rearrange("p a (b ph t) -> p (a b) t ph", b=2, t=4))
         wg_perm = []
 
         def permute_wg(b):
-            perm = sb(f"wg_perm{b}", [P, 2, 4, 64], I32)
+            perm = sb(f"wg_perm{b}", [P, 2, 4, 64], I32, tag=f"slot_perm{b}")
             nc.vector.tensor_copy(
                 perm[:].rearrange("p a t (ph e) -> p a t ph e", e=2),
                 wg_raw[:, :, 256 * b : 256 * (b + 1)].rearrange("p a (ph t e) -> p a t ph e", t=4, e=2),
             )
             wg_perm.append(perm)
 
-        gather_words(0)
-        load_wv(1, 0, "slot_picked0")
         permute_wg(0)
-        gather_words(1)
         permute_wg(1)
-        load_wv(1, 1, "slot_words")
+        wv_first = sb("wv_first", [P, 2, 4, 512], F32, tag="slot_wg")
+        load_wv(0, 0, wv_first[:, 0])
+        load_wv(0, 1, wv_first[:, 1])
+        wgs = sb("wgs", [P, 4, 4, 32], I32)
+        nc.vector.tensor_copy(wgs[:], wgs_raw[:].rearrange("p a (b ph t) -> p (a b) t ph", b=2, t=4))
+        gather_words(0)
+        load_wv(1, 0, sb("wv_raw10", [P, 4, 512], F32, tag="slot_picked0")[:])
+        gather_words(1)
+        load_wv(1, 1, sb("wv_raw11", [P, 4, 512], F32, tag="slot_words")[:])
+        bo_cols = sb("bo_cols", [P, 4], F32, tag="slot_picked1")
+        with nc.allow_non_contiguous_dma(reason="one bias value a partition"):
+            nc.sync.dma_start(bo_cols[:], bo.rearrange("(c p) -> p c", p=P))
 
         gate = {}
 
@@ -137,9 +142,9 @@ def tile_list_gated_click_interests_kernel(tc, tab, offs, wv, wg_words, wg_scale
         wv_bf, wv_codes, wv_scales = {}, {}, {}
 
         def round_wv(b, a, on_vector):
-            bf = sb(f"wv_bf{b}{a}", [P, 4, 512], BF16)
+            bf = sb(f"wv_bf{b}{a}", [P, 4, 512], BF16, tag="slot_perm0" if (b, a) == (1, 1) else f"slot_bf{b}{a}")
             dst = bf[:].rearrange("p t (ph el j) -> p t ph j el", el=4, j=4)
-            src = wv_raw[b, a][:].rearrange("p j (ph t el) -> p t ph j el", t=4, el=4)
+            src = wv_raw[b, a].rearrange("p j (ph t el) -> p t ph j el", t=4, el=4)
             if on_vector:
                 nc.vector.tensor_copy(dst, src)
             else:
@@ -156,7 +161,7 @@ def tile_list_gated_click_interests_kernel(tc, tab, offs, wv, wg_words, wg_scale
                 in_=wv_bf[b, a][:].rearrange("p t c -> p (t c)"),
             )
 
-        h_bf = {}
+        h_bf = [sb(f"h_bf{b}", [P, 4 * S], BF16) for b in range(2)]
         h_codes = [sb(f"h_codes{b}", [P, S], U32) for b in range(2)]
         h_scales = [sb(f"h_scales{b}", [P, S], U8) for b in range(2)]
 
@@ -174,17 +179,18 @@ def tile_list_gated_click_interests_kernel(tc, tab, offs, wv, wg_words, wg_scale
                         start=(a == 0),
                         stop=(a == 1),
                     )
-            h_bf[b, jc] = sb(f"h_bf{b}{jc}", [P, 4 * CH], BF16)
             nc.vector.tensor_tensor(
-                h_bf[b, jc][:].rearrange("p (c i t) -> p c t i", i=4, t=4),
+                h_bf[b][:, 4 * CH * jc : 4 * CH * (jc + 1)].rearrange("p (c i t) -> p c t i", i=4, t=4),
                 val[:].rearrange("p t (c i) -> p c t i", i=4),
                 gate[b, jh][:, :, j0 : j0 + CH].rearrange("p t (c i) -> p c t i", i=4),
                 ALU.mult,
             )
 
-        def quantise_h(b, jc):
-            cols = slice(jc * CH, (jc + 1) * CH)
-            nc.vector.quantize_mx(out=h_codes[b][:, cols].bitcast(FP8X4), scales=h_scales[b][:, cols], in_=h_bf[b, jc][:])
+        def quantise_h(b, jc, chunks):
+            j0, j1 = jc * CH, (jc + chunks) * CH
+            nc.vector.quantize_mx(
+                out=h_codes[b][:, j0:j1].bitcast(FP8X4), scales=h_scales[b][:, j0:j1], in_=h_bf[b][:, 4 * j0 : 4 * j1]
+            )
 
         wo_raw, wo_codes, wo_scales, wo_bf = {}, {}, {}, {}
 
@@ -195,13 +201,13 @@ def tile_list_gated_click_interests_kernel(tc, tab, offs, wv, wg_words, wg_scale
                 nc.sync.dma_start(raw[:, t, :], rows[t])
             wo_raw[b] = raw
 
-        def round_wo(b, half):
-            if half == 0:
-                wo_bf[b] = sb(f"wo_bf{b}", [P, 4 * N], BF16)
-            nc.scalar.copy(
-                wo_bf[b][:, 1024 * half : 1024 * (half + 1)].rearrange("p (c i t) -> p c t i", i=4, t=4),
-                wo_raw[b][:, :, 256 * half : 256 * (half + 1)].rearrange("p t (c i) -> p c t i", i=4),
-            )
+        def round_wo(b):
+            wo_bf[b] = sb(f"wo_bf{b}", [P, 4 * N], BF16)
+            for half in range(2):
+                nc.scalar.copy(
+                    wo_bf[b][:, 1024 * half : 1024 * (half + 1)].rearrange("p (c i t) -> p c t i", i=4, t=4),
+                    wo_raw[b][:, :, 256 * half : 256 * (half + 1)].rearrange("p t (c i) -> p c t i", i=4),
+                )
 
         def quantise_wo(b):
             wo_codes[b] = sb(f"wo_codes{b}", [P, N], U32)
@@ -228,9 +234,9 @@ def tile_list_gated_click_interests_kernel(tc, tab, offs, wv, wg_words, wg_scale
                             start=(b == 0),
                             stop=(b == 1),
                         )
-                on_vector = index == len(PIECES) - 1 and nt0 == 0
+                on_vector = index == 4 and nt0 == 0
                 for i in range(per_bank):
-                    bias = bias_cols[:, 0, 4 + nt0 + i : 5 + nt0 + i]
+                    bias = bo_cols[:, nt0 + i : nt0 + i + 1]
                     if on_vector:
                         nc.vector.tensor_scalar(res[:, i, :], acc[:, i, :], bias, None, ALU.add)
                     else:
@@ -242,35 +248,35 @@ def tile_list_gated_click_interests_kernel(tc, tab, offs, wv, wg_words, wg_scale
                 gate_tile(0, jh, t)
         round_wv(0, 0, True)
         quantise_wv(0, 0)
-        load_wo(0, "slot_a")
         round_wv(0, 1, True)
+        load_wo(0, "slot_wg")
         quantise_wv(0, 1)
-        load_wo(1, "slot_scales")
+        load_wo(1, "slot_bf01")
+        round_wv(1, 0, True)
         for jc in range(8):
-            value_chunk(0, jc)
             gate_tile(1, jc // 4, jc % 4)
-            if jc == 1:
-                round_wv(1, 0, False)
-            if jc == 2:
+            value_chunk(0, jc)
+            if jc == 0:
                 quantise_wv(1, 0)
-            if jc == 4:
+            if jc == 3:
                 round_wv(1, 1, False)
             if jc == 5:
                 quantise_wv(1, 1)
-            if jc > 0:
-                quantise_h(0, jc - 1)
+            if jc in (2, 4, 6):
+                quantise_h(0, jc - 2, 2)
         for b in range(2):
-            for half in range(2):
-                round_wo(b, half)
+            round_wo(b)
         for jc in range(8):
             value_chunk(1, jc)
-            quantise_h(*((0, 7) if jc == 0 else (1, jc - 1)))
-            if jc in (1, 2):
-                quantise_wo(jc - 1)
-            if jc == 4:
-                out_piece(0)
-            if jc == 6:
-                out_piece(1)
-        out_piece(2)
-        quantise_h(1, 7)
+            if jc == 0:
+                quantise_wo(0)
+                quantise_h(0, 6, 2)
+            if jc == 1:
+                quantise_wo(1)
+            if jc in (2, 4, 6):
+                quantise_h(1, jc - 2, 2)
+                out_piece(jc // 2 - 1)
+        quantise_h(1, 6, 1)
         out_piece(3)
+        quantise_h(1, 7, 1)
+        out_piece(4)

@@ -18,17 +18,23 @@ ACT = mybir.ActivationFunctionType
 ALU = mybir.AluOpType
 
 P = 128
+PASS = 512
 HALF = 512
-CH = 128
+CHUNK = 128
+CHUNKS = S // CHUNK
 PIECES = [(0, 256), (256, 256), (512, 256), (768, 128), (896, 128)]
+ZERO_SPLIT = 640
+PASS1_SHIFT = 16
+WIDE_BANKS, VALUE_BANKS = 5, 3
+WARM_PASSES = 3
 
 
 def tile_list_gated_click_interests_kernel(tc, tab, offs, wv, wg_words, wg_scales, bg, wo, bo, out):
     nc = tc.nc
     with ExitStack() as ctx:
         keep = ctx.enter_context(tc.tile_pool(name="keep", bufs=1))
-        bank_wide = ctx.enter_context(tc.psum_pool(name="bank_wide", bufs=5))
-        bank_val = ctx.enter_context(tc.psum_pool(name="bank_val", bufs=3))
+        wide_banks = ctx.enter_context(tc.psum_pool(name="wide_banks", bufs=WIDE_BANKS))
+        value_banks = ctx.enter_context(tc.psum_pool(name="value_banks", bufs=VALUE_BANKS))
 
         def sb(name, shape, dt, tag=None):
             return keep.tile(shape, dt, name=name, tag=tag or name, align_bytes=64)
@@ -37,246 +43,263 @@ def tile_list_gated_click_interests_kernel(tc, tab, offs, wv, wg_words, wg_scale
         nc.sync.dma_start(offsets[:], offs)
 
         tab32 = tab.bitcast(I32)
-        tab_scales = sb("tab_scales", [P, T // 4], I32, tag="slot_wg")
-        nc.vector.memset(tab_scales[:, 0:640], 0)
-        nc.gpsimd.memset(tab_scales[:, 640:1024], 0)
-        bias_rows = sb("bias_rows", [P, 2, P], F32)
+        tab_scales = sb("tab_scales", [P, T // 4], I32, tag="after_scale_gather")
+        nc.vector.memset(tab_scales[:, 0:ZERO_SPLIT], 0)
+        nc.gpsimd.memset(tab_scales[:, ZERO_SPLIT:], 0)
+
+        bias_rows = sb("bias_rows", [P, 4, P], F32)
         nc.gpsimd.memset(bias_rows[:], 0.0)
-        nc.scalar.dma_start(
-            bias_rows[0:4].rearrange("t b (ph el) -> t (b ph) el", el=4),
-            bg.rearrange("(x t el) -> t x el", t=4, el=4),
-        )
+        bg_rows = sb("bg_rows", [2, PASS], F32)
+        nc.scalar.dma_start(bg_rows[:], bg.rearrange("(b c) -> b c", b=2))
         identity = sb("identity", [P, P], F32)
         make_identity(nc, identity[:])
-        warm = sb("warm", [P, 1], F32)
-        nc.scalar.activation(warm[:], identity[:, 0:1], ACT.Sigmoid)
-        wg_raw = sb("wg_raw", [P, 2, 512], I32)
-        for a in range(2):
-            nc.sync.dma_start(wg_raw[:, a, :], wg_words.bitcast(I32)[a])
-        scale_rows = tab32[0, P * T :].rearrange("(h q r t) -> r q h t", h=2, q=4, r=4)
+
+        warm_column = sb("warm_column", [P, 1], F32)
+        nc.scalar.activation(warm_column[:], identity[:, 0:1], ACT.Sigmoid)
+
+        wg_raw = sb("wg_raw", [P, 2, H // 2], I32)
+        nc.sync.dma_start(wg_raw[:], wg_words.bitcast(I32).rearrange("a p w -> p a w"))
+        scale_rows = tab32[0, P * T :].rearrange("(a q r t) -> r q a t", a=2, q=4, r=4)
         for r in range(4):
-            nc.sync.dma_start(tab_scales[r:P:16, :], scale_rows[r])
-        tab_words = sb("tab_words", [P, T], I32, tag="slot_words")
+            nc.sync.dma_start(tab_scales[r:P:PASS1_SHIFT, :], scale_rows[r])
+        tab_words = sb("tab_words", [P, T], I32, tag="after_word_gathers")
         nc.sync.dma_start(tab_words[:], tab32[0, 0 : P * T].rearrange("(p t) -> p t", p=P))
 
-        wgs_raw = sb("wgs_raw", [P, 2, 256], I32, tag="slot_wgs")
-        nc.vector.memset(wgs_raw[:], 0)
-        wgs32 = wg_scales.bitcast(I32)
+        wg_planes_raw = sb("wg_planes_raw", [P, 2, H // 4], I32, tag="after_wg_planes")
+        nc.vector.memset(wg_planes_raw[:], 0)
+        wg_scales32 = wg_scales.bitcast(I32)
         for q in range(4):
-            nc.gpsimd.dma_start(wgs_raw[32 * q : 32 * q + 4, :, :], wgs32[:, 4 * q : 4 * q + 4, :].rearrange("a r w -> r a w"))
+            nc.sync.dma_start(
+                wg_planes_raw[32 * q : 32 * q + 4, :, :],
+                wg_scales32[:, 4 * q : 4 * q + 4, :].rearrange("a r w -> r a w"),
+            )
 
-        picked_scales1 = sb("picked_scales1", [P, S // 4], I32)
-        nc.vector.memset(picked_scales1[:], 0)
+        nc.sync.dma_start(bias_rows[2:3].rearrange("o c p -> o (c p)"), bo.rearrange("(o n) -> o n", o=1))
+        plane1 = sb("plane1", [P, S // 4], I32)
+        nc.vector.memset(plane1[:], 0)
 
-        turned = bank_wide.tile([P, 2, P], F32, name="wide")
-        for b in range(2):
-            nc.tensor.transpose(turned[:, b, :], bias_rows[:, b, :], identity[:])
-        bias_cols = sb("bias_cols", [P, 2, 4], F32)
-        nc.vector.tensor_copy(bias_cols[:], turned[:, :, 0:4])
+        nc.scalar.copy(
+            bias_rows[0:2].rearrange("b t (ph el) -> b t ph el", el=4),
+            bg_rows[:].rearrange("b (ph t el) -> b t ph el", t=4, el=4),
+        )
+        turned = wide_banks.tile([P, 4, P], F32, name="wide")
+        for t in range(4):
+            nc.tensor.transpose(turned[:, t, :], bias_rows[:, t, :], identity[:])
+        bias_cols = sb("bias_cols", [P, 4, 3], F32)
+        nc.scalar.copy(bias_cols[:], turned[:, :, 0:3])
 
-        wv_raw = {}
+        plane0 = sb("plane0", [P, S], U8)
+        nc.vector.tensor_copy(plane0[:], tab_scales[:].bitcast(U8).indirect(offsets[:]))
+        nc.sync.dma_start(plane1[0 : P - PASS1_SHIFT, :], plane0[:].bitcast(I32)[PASS1_SHIFT:P, :])
+        picked_planes = [plane0[:], plane1[:].bitcast(U8)]
+
+        wv_raw, picked_codes, wg_codes = {}, [], []
 
         def load_wv(b, a, raw):
-            nc.sync.dma_start(raw, wv[512 * a : 512 * (a + 1), 512 * b : 512 * (b + 1)].rearrange("(p j) c -> p j c", j=4))
+            rows, cols = slice(PASS * a, PASS * (a + 1)), slice(PASS * b, PASS * (b + 1))
+            nc.sync.dma_start(raw, wv[rows, cols].rearrange("(p i) c -> p i c", i=4))
             wv_raw[b, a] = raw
 
-
-        picked_scales0 = sb("picked_scales0", [P, S], U8)
-        nc.vector.tensor_copy(picked_scales0[:], tab_scales[:].bitcast(U8).indirect(offsets[:]))
-        nc.sync.dma_start(picked_scales1[0:112, :], picked_scales0[:].bitcast(I32)[16:128, :])
-        tab_planes = [picked_scales0[:], picked_scales1[:].bitcast(U8)]
-
-
-        parted = []
-
-        def gather_words(jh):
-            picked = sb(f"picked{jh}", [P, HALF], U32, tag=f"slot_picked{jh}")
-            nc.vector.tensor_copy(picked[:], tab_words[:].bitcast(U32).indirect(offsets[:, 32 * jh : 32 * (jh + 1)]))
-            part = sb(f"parted{jh}", [P, 2, 2 * HALF], U8)
-            nc.vector.tensor_copy(part[:].bitcast(U16), picked[:].bitcast(U16).rearrange("p (j h) -> p h j", h=2))
-            parted.append(part)
-
-        wg_perm = []
+        def gather_words(half, tag):
+            picked = sb(f"picked{half}", [P, HALF], U32, tag=tag)
+            list_cols = slice(HALF // 16 * half, HALF // 16 * (half + 1))
+            nc.vector.tensor_copy(picked[:], tab_words[:].bitcast(U32).indirect(offsets[:, list_cols]))
+            parted = sb(f"parted{half}", [P, 2, 2 * HALF], U8)
+            nc.vector.tensor_copy(parted[:].bitcast(U16), picked[:].bitcast(U16).rearrange("p (j a) -> p a j", a=2))
+            picked_codes.append(parted)
 
         def permute_wg(b):
-            perm = sb(f"wg_perm{b}", [P, 2, 4, 64], I32, tag=f"slot_perm{b}")
+            codes = sb(f"wg_codes{b}", [P, 2, 4, P // 2], I32, tag=f"after_gates{b}")
             nc.vector.tensor_copy(
-                perm[:].rearrange("p a t (ph e) -> p a t ph e", e=2),
+                codes[:].rearrange("p a t (ph e) -> p a t ph e", e=2),
                 wg_raw[:, :, 256 * b : 256 * (b + 1)].rearrange("p a (ph t e) -> p a t ph e", t=4, e=2),
             )
-            wg_perm.append(perm)
+            wg_codes.append(codes)
 
         permute_wg(0)
         permute_wg(1)
-        wv_first = sb("wv_first", [P, 2, 4, 512], F32, tag="slot_wg")
+        wv_first = sb("wv_first", [P, 2, 4, PASS], F32, tag="after_scale_gather")
         load_wv(0, 0, wv_first[:, 0])
         load_wv(0, 1, wv_first[:, 1])
-        wgs = sb("wgs", [P, 4, 4, 32], I32)
-        nc.vector.tensor_copy(wgs[:], wgs_raw[:].rearrange("p a (b ph t) -> p (a b) t ph", b=2, t=4))
-        gather_words(0)
-        load_wv(1, 0, sb("wv_raw10", [P, 4, 512], F32, tag="slot_picked0")[:])
-        gather_words(1)
-        load_wv(1, 1, sb("wv_raw11", [P, 4, 512], F32, tag="slot_words")[:])
-        bo_cols = sb("bo_cols", [P, 4], F32, tag="slot_picked1")
-        with nc.allow_non_contiguous_dma(reason="one bias value a partition"):
-            nc.sync.dma_start(bo_cols[:], bo.rearrange("(c p) -> p c", p=P))
+        gather_words(0, "after_first_parting")
+
+        warm_bank = wide_banks.tile([P, HALF], F32, name="wide")
+        for t in range(WARM_PASSES):
+            nc.tensor.matmul_mx(
+                out=warm_bank[:],
+                lhsT=wg_codes[0][:, 0, t, :].bitcast(FP4X4),
+                lhsT_scale=wg_planes_raw[:, 0, 0 : P // 4].bitcast(U8),
+                rhs=wg_raw[:, 0, 0 : HALF // 2].bitcast(FP4X4),
+                rhs_scale=wg_planes_raw[:, 0, 0 : HALF // 4].bitcast(U8),
+                start=True,
+                stop=True,
+            )
+
+        wg_planes = sb("wg_planes", [P, 4, 4, P // 4], I32, tag="after_first_parting")
+        nc.vector.tensor_copy(wg_planes[:], wg_planes_raw[:].rearrange("p a (b ph t) -> p (a b) t ph", b=2, t=4))
+        gather_words(1, "after_wg_planes")
+        load_wv(1, 0, sb("wv_raw10", [P, 4, PASS], F32, tag="after_word_gathers")[:])
+        load_wv(1, 1, sb("wv_raw11", [P, 4, PASS], F32, tag="after_wg_planes")[:])
 
         gate = {}
 
-        def gate_tile(b, jh, t):
+        def gate_tile(b, half, t):
             if t == 0:
-                gate[b, jh] = sb(f"gate{b}{jh}", [P, 4, HALF], F32)
-            z = bank_wide.tile([P, HALF], F32, name="wide")
+                gate[b, half] = sb(f"gate{b}{half}", [P, 4, HALF], F32)
+            z = wide_banks.tile([P, HALF], F32, name="wide")
             for a in range(2):
                 nc.tensor.matmul_mx(
                     out=z[:],
-                    lhsT=wg_perm[b][:, a, t, :].bitcast(FP4X4),
-                    lhsT_scale=wgs[:, 2 * a + b, t, :].bitcast(U8),
-                    rhs=parted[jh][:, a, :].bitcast(FP4X4),
-                    rhs_scale=tab_planes[a][:, HALF * jh : HALF * (jh + 1)],
+                    lhsT=wg_codes[b][:, a, t, :].bitcast(FP4X4),
+                    lhsT_scale=wg_planes[:, 2 * a + b, t, :].bitcast(U8),
+                    rhs=picked_codes[half][:, a, :].bitcast(FP4X4),
+                    rhs_scale=picked_planes[a][:, HALF * half : HALF * (half + 1)],
                     start=(a == 0),
                     stop=(a == 1),
                 )
-            nc.scalar.activation(gate[b, jh][:, t, :], z[:], ACT.Sigmoid, bias=bias_cols[:, b, t : t + 1])
+            nc.scalar.activation(gate[b, half][:, t, :], z[:], ACT.Sigmoid, bias=bias_cols[:, t, b : b + 1])
 
-        wv_bf, wv_codes, wv_scales = {}, {}, {}
+        wv_bf, wv_codes, wv_planes = {}, {}, {}
 
-        def round_wv(b, a, on_vector):
-            bf = sb(f"wv_bf{b}{a}", [P, 4, 512], BF16, tag="slot_perm0" if (b, a) == (1, 1) else f"slot_bf{b}{a}")
-            dst = bf[:].rearrange("p t (ph el j) -> p t ph j el", el=4, j=4)
-            src = wv_raw[b, a].rearrange("p j (ph t el) -> p t ph j el", t=4, el=4)
-            if on_vector:
-                nc.vector.tensor_copy(dst, src)
-            else:
-                for t in range(4):
-                    nc.scalar.copy(dst[:, t], src[:, t])
-            wv_bf[b, a] = bf
+        def wv_rounding_views(b, a, tag):
+            wv_bf[b, a] = sb(f"wv_bf{b}{a}", [P, 4, PASS], BF16, tag=tag)
+            return (
+                wv_bf[b, a][:].rearrange("p t (ph el i) -> p t ph i el", el=4, i=4),
+                wv_raw[b, a].rearrange("p i (ph t el) -> p t ph i el", t=4, el=4),
+            )
+
+        def round_wv_on_vector(b, a):
+            dst, src = wv_rounding_views(b, a, f"after_quantise_wv{b}{a}")
+            nc.vector.tensor_copy(dst, src)
+
+        def round_wv_on_scalar(b, a):
+            dst, src = wv_rounding_views(b, a, "after_gates0")
+            for t in range(4):
+                nc.scalar.copy(dst[:, t], src[:, t])
 
         def quantise_wv(b, a):
-            wv_codes[b, a] = sb(f"wv_codes{b}{a}", [P, 512], U32)
-            wv_scales[b, a] = sb(f"wv_scales{b}{a}", [P, 512], U8)
+            wv_codes[b, a] = sb(f"wv_codes{b}{a}", [P, PASS], U32)
+            wv_planes[b, a] = sb(f"wv_planes{b}{a}", [P, PASS], U8)
             nc.vector.quantize_mx(
                 out=wv_codes[b, a][:].bitcast(FP8X4),
-                scales=wv_scales[b, a][:],
+                scales=wv_planes[b, a][:],
                 in_=wv_bf[b, a][:].rearrange("p t c -> p (t c)"),
             )
 
         h_bf = [sb(f"h_bf{b}", [P, 4 * S], BF16) for b in range(2)]
         h_codes = [sb(f"h_codes{b}", [P, S], U32) for b in range(2)]
-        h_scales = [sb(f"h_scales{b}", [P, S], U8) for b in range(2)]
+        h_planes = [sb(f"h_planes{b}", [P, S], U8) for b in range(2)]
 
-        def value_chunk(b, jc):
-            jh, j0 = divmod(jc * CH, HALF)
-            val = bank_val.tile([P, 4, CH], F32, name="val")
+        def value_chunk(b, chunk):
+            half, j0 = divmod(chunk * CHUNK, HALF)
+            val = value_banks.tile([P, 4, CHUNK], F32, name="val")
             for t in range(4):
                 for a in range(2):
                     nc.tensor.matmul_mx(
                         out=val[:, t, :],
                         lhsT=wv_codes[b, a][:, P * t : P * (t + 1)].bitcast(FP8X4),
-                        lhsT_scale=wv_scales[b, a][:, P * t : P * (t + 1)],
-                        rhs=parted[jh][:, a, 2 * j0 : 2 * (j0 + CH)].bitcast(FP4X4),
-                        rhs_scale=tab_planes[a][:, jc * CH : (jc + 1) * CH],
+                        lhsT_scale=wv_planes[b, a][:, P * t : P * (t + 1)],
+                        rhs=picked_codes[half][:, a, 2 * j0 : 2 * (j0 + CHUNK)].bitcast(FP4X4),
+                        rhs_scale=picked_planes[a][:, chunk * CHUNK : (chunk + 1) * CHUNK],
                         start=(a == 0),
                         stop=(a == 1),
                     )
             nc.vector.tensor_tensor(
-                h_bf[b][:, 4 * CH * jc : 4 * CH * (jc + 1)].rearrange("p (c i t) -> p c t i", i=4, t=4),
-                val[:].rearrange("p t (c i) -> p c t i", i=4),
-                gate[b, jh][:, :, j0 : j0 + CH].rearrange("p t (c i) -> p c t i", i=4),
+                h_bf[b][:, 4 * CHUNK * chunk : 4 * CHUNK * (chunk + 1)].rearrange("p (c u t) -> p c t u", u=4, t=4),
+                val[:].rearrange("p t (c u) -> p c t u", u=4),
+                gate[b, half][:, :, j0 : j0 + CHUNK].rearrange("p t (c u) -> p c t u", u=4),
                 ALU.mult,
             )
 
-        def quantise_h(b, jc, chunks):
-            j0, j1 = jc * CH, (jc + chunks) * CH
+        def quantise_h(b, first_chunk, chunks):
+            j0, j1 = first_chunk * CHUNK, (first_chunk + chunks) * CHUNK
             nc.vector.quantize_mx(
-                out=h_codes[b][:, j0:j1].bitcast(FP8X4), scales=h_scales[b][:, j0:j1], in_=h_bf[b][:, 4 * j0 : 4 * j1]
+                out=h_codes[b][:, j0:j1].bitcast(FP8X4), scales=h_planes[b][:, j0:j1], in_=h_bf[b][:, 4 * j0 : 4 * j1]
             )
 
-        wo_raw, wo_codes, wo_scales, wo_bf = {}, {}, {}, {}
+        wo_raw, wo_bf, wo_codes, wo_planes = {}, {}, {}, {}
 
         def load_wo(b, tag):
-            raw = sb(f"wo_raw{b}", [P, 4, N], F32, tag=tag)
-            rows = wo[512 * b : 512 * (b + 1), :].rearrange("(ph t el) n -> t ph el n", t=4, el=4)
+            wo_raw[b] = sb(f"wo_raw{b}", [P, 4, N], F32, tag=tag)
+            rows = wo[PASS * b : PASS * (b + 1), :].rearrange("(ph t el) n -> t ph el n", t=4, el=4)
             for t in range(4):
-                nc.sync.dma_start(raw[:, t, :], rows[t])
-            wo_raw[b] = raw
+                nc.sync.dma_start(wo_raw[b][:, t, :], rows[t])
 
         def round_wo(b):
             wo_bf[b] = sb(f"wo_bf{b}", [P, 4 * N], BF16)
-            for half in range(2):
+            for n0 in range(0, N, N // 2):
                 nc.scalar.copy(
-                    wo_bf[b][:, 1024 * half : 1024 * (half + 1)].rearrange("p (c i t) -> p c t i", i=4, t=4),
-                    wo_raw[b][:, :, 256 * half : 256 * (half + 1)].rearrange("p t (c i) -> p c t i", i=4),
+                    wo_bf[b][:, 4 * n0 : 4 * (n0 + N // 2)].rearrange("p (c u t) -> p c t u", u=4, t=4),
+                    wo_raw[b][:, :, n0 : n0 + N // 2].rearrange("p t (c u) -> p c t u", u=4),
                 )
 
         def quantise_wo(b):
             wo_codes[b] = sb(f"wo_codes{b}", [P, N], U32)
-            wo_scales[b] = sb(f"wo_scales{b}", [P, N], U8)
-            nc.vector.quantize_mx(out=wo_codes[b][:].bitcast(FP8X4), scales=wo_scales[b][:], in_=wo_bf[b][:])
+            wo_planes[b] = sb(f"wo_planes{b}", [P, N], U8)
+            nc.vector.quantize_mx(out=wo_codes[b][:].bitcast(FP8X4), scales=wo_planes[b][:], in_=wo_bf[b][:])
 
         out_rows = out.rearrange("(nt p) j -> p nt j", p=P)
 
         def out_piece(index):
             j0, width = PIECES[index]
-            per_bank = 1 if width == 512 else 2
-            for nt0 in range(0, 4, per_bank):
-                acc = bank_wide.tile([P, per_bank, width], F32, name="wide")
-                res = sb(f"res{index}{nt0}", [P, per_bank, width], F32)
-                for i in range(per_bank):
-                    cols = slice(P * (nt0 + i), P * (nt0 + i + 1))
+            for nt0 in (0, 2):
+                acc = wide_banks.tile([P, 2, width], F32, name="wide")
+                res = sb(f"res{index}{nt0}", [P, 2, width], F32)
+                for slot in range(2):
+                    cols = slice(P * (nt0 + slot), P * (nt0 + slot + 1))
                     for b in range(2):
                         nc.tensor.matmul_mx(
-                            out=acc[:, i, :],
+                            out=acc[:, slot, :],
                             lhsT=wo_codes[b][:, cols].bitcast(FP8X4),
-                            lhsT_scale=wo_scales[b][:, cols],
+                            lhsT_scale=wo_planes[b][:, cols],
                             rhs=h_codes[b][:, j0 : j0 + width].bitcast(FP8X4),
-                            rhs_scale=h_scales[b][:, j0 : j0 + width],
+                            rhs_scale=h_planes[b][:, j0 : j0 + width],
                             start=(b == 0),
                             stop=(b == 1),
                         )
-                on_vector = index == 4 and nt0 == 0
-                for i in range(per_bank):
-                    bias = bo_cols[:, nt0 + i : nt0 + i + 1]
+                on_vector = index == len(PIECES) - 1 and nt0 == 0
+                for slot in range(2):
+                    bias = bias_cols[:, nt0 + slot, 2:3]
                     if on_vector:
-                        nc.vector.tensor_scalar(res[:, i, :], acc[:, i, :], bias, None, ALU.add)
+                        nc.vector.tensor_scalar(res[:, slot, :], acc[:, slot, :], bias, None, ALU.add)
                     else:
-                        nc.scalar.activation(res[:, i, :], acc[:, i, :], ACT.Identity, bias=bias)
-                nc.sync.dma_start(out_rows[:, nt0 : nt0 + per_bank, j0 : j0 + width], res[:])
+                        nc.scalar.activation(res[:, slot, :], acc[:, slot, :], ACT.Identity, bias=bias)
+                nc.sync.dma_start(out_rows[:, nt0 : nt0 + 2, j0 : j0 + width], res[:])
 
-        for jh in range(2):
+        for half in range(2):
             for t in range(4):
-                gate_tile(0, jh, t)
-        round_wv(0, 0, True)
+                gate_tile(0, half, t)
+        round_wv_on_vector(0, 0)
         quantise_wv(0, 0)
-        round_wv(0, 1, True)
-        load_wo(0, "slot_wg")
+        round_wv_on_vector(0, 1)
+        load_wo(0, "after_scale_gather")
         quantise_wv(0, 1)
-        load_wo(1, "slot_bf01")
-        round_wv(1, 0, True)
-        for jc in range(8):
-            gate_tile(1, jc // 4, jc % 4)
-            value_chunk(0, jc)
-            if jc == 0:
-                quantise_wv(1, 0)
-            if jc == 3:
-                round_wv(1, 1, False)
-            if jc == 5:
-                quantise_wv(1, 1)
-            if jc in (2, 4, 6):
-                quantise_h(0, jc - 2, 2)
+        load_wo(1, "after_quantise_wv01")
+        round_wv_on_vector(1, 0)
+
+        between_chunks = {0: (quantise_wv, 1, 0), 3: (round_wv_on_scalar, 1, 1), 5: (quantise_wv, 1, 1)}
+        for chunk in range(CHUNKS):
+            gate_tile(1, chunk // 4, chunk % 4)
+            value_chunk(0, chunk)
+            if chunk in between_chunks:
+                step, b, a = between_chunks[chunk]
+                step(b, a)
+            if chunk > 0 and chunk % 2 == 0:
+                quantise_h(0, chunk - 2, 2)
         for b in range(2):
             round_wo(b)
-        for jc in range(8):
-            value_chunk(1, jc)
-            if jc == 0:
-                quantise_wo(0)
-                quantise_h(0, 6, 2)
-            if jc == 1:
-                quantise_wo(1)
-            if jc in (2, 4, 6):
-                quantise_h(1, jc - 2, 2)
-                out_piece(jc // 2 - 1)
-        quantise_h(1, 6, 1)
-        out_piece(3)
-        quantise_h(1, 7, 1)
-        out_piece(4)
+
+        value_chunk(1, 0)
+        quantise_wo(0)
+        quantise_h(0, CHUNKS - 2, 2)
+        value_chunk(1, 1)
+        quantise_wo(1)
+        for chunk in range(2, CHUNKS):
+            value_chunk(1, chunk)
+            if chunk % 2 == 0:
+                quantise_h(1, chunk - 2, 2)
+                out_piece(chunk // 2 - 1)
+        quantise_h(1, CHUNKS - 2, 1)
+        out_piece(len(PIECES) - 2)
+        quantise_h(1, CHUNKS - 1, 1)
+        out_piece(len(PIECES) - 1)

@@ -23,85 +23,99 @@ HALF = 512
 CHUNK = 128
 CHUNKS = S // CHUNK
 PIECES = [(0, 256), (256, 256), (512, 256), (768, 128), (896, 128)]
-ZERO_SPLIT = 640
-PASS1_SHIFT = 16
-WIDE_BANKS, VALUE_BANKS = 5, 3
+SCALE_ROWS = 32
+RAW = 4 * PASS * 4
+BANKS, BANK_BYTES = 8, 2048
 WARM_PASSES = 3
+EARLY_GATES = 11
+WO_STEP = 128
+BO_ROW = 32
 
 
 def tile_list_gated_click_interests_kernel(tc, tab, offs, wv, wg_words, wg_scales, bg, wo, bo, out):
     nc = tc.nc
     with ExitStack() as ctx:
         keep = ctx.enter_context(tc.tile_pool(name="keep", bufs=1))
-        wide_banks = ctx.enter_context(tc.psum_pool(name="wide_banks", bufs=WIDE_BANKS))
-        value_banks = ctx.enter_context(tc.psum_pool(name="value_banks", bufs=VALUE_BANKS))
+        turns = ctx.enter_context(tc.tile_pool(name="turns", bufs=1))
+        psum = ctx.enter_context(tc.psum_pool(name="psum", bufs=1))
+        banks_taken = []
+
+        def next_bank(shape):
+            turn = len(banks_taken)
+            banks_taken.append(turn)
+            return psum.tile(shape, F32, name=f"sums{turn}", offset=BANK_BYTES * (turn % BANKS))
 
         def sb(name, shape, dt, tag=None):
             return keep.tile(shape, dt, name=name, tag=tag or name, align_bytes=64)
+
+        def placed(name, shape, dt, offset):
+            return turns.tile(shape, dt, name=name, align_bytes=64, offset=offset)
 
         offsets = keep.tile([P, S // 16], U16, name="offsets")
         nc.sync.dma_start(offsets[:], offs)
 
         tab32 = tab.bitcast(I32)
-        tab_scales = sb("tab_scales", [P, T // 4], I32, tag="after_scale_gather")
-        nc.vector.memset(tab_scales[:, 0:ZERO_SPLIT], 0)
-        nc.gpsimd.memset(tab_scales[:, ZERO_SPLIT:], 0)
+        tab_scales = sb("tab_scales", [P, T // 4], I32)
+        nc.sync.dma_start(
+            tab_scales[0:SCALE_ROWS, :], tab32[0, P * T :].rearrange("(a r t) -> r a t", a=2, r=16)
+        )
+        wg_scale_rows = sb("wg_scale_rows", [SCALE_ROWS, H // 4], I32)
+        nc.sync.dma_start(wg_scale_rows[:], wg_scales.bitcast(I32).rearrange("a r w -> r a w"))
+        tab_words = placed("tab_words", [P, T], I32, 2 * RAW)
+        nc.sync.dma_start(tab_words[:], tab32[0, 0 : P * T].rearrange("(p t) -> p t", p=P))
+        wg32 = wg_words.bitcast(I32).rearrange("a p w -> p a w")
+        wg_raw = [placed("wg_raw0", [P, 2, 256], I32, 4 * RAW + 2048), sb("wg_raw1", [P, 2, 256], I32)]
+        for b in range(2):
+            nc.sync.dma_start(wg_raw[b][:], wg32[:, :, 256 * b : 256 * (b + 1)])
 
+        nc.vector.memset(tab_scales[32:64, :], 0)
+        nc.gpsimd.memset(tab_scales[64:P, :], 0)
+        planes = sb("planes", [P, 2, (S + H) // 4], I32)
+        nc.vector.memset(planes[:], 0)
+
+        bias_in = sb("bias_in", [BO_ROW + 1, PASS], F32)
+        nc.scalar.dma_start(bias_in[0:2], bg.rearrange("(b c) -> b c", b=2))
+        nc.scalar.dma_start(bias_in[BO_ROW : BO_ROW + 1], bo.rearrange("(o n) -> o n", o=1))
         bias_rows = sb("bias_rows", [P, 4, P], F32)
         nc.gpsimd.memset(bias_rows[:], 0.0)
-        bg_rows = sb("bg_rows", [2, PASS], F32)
-        nc.scalar.dma_start(bg_rows[:], bg.rearrange("(b c) -> b c", b=2))
         identity = sb("identity", [P, P], F32)
         make_identity(nc, identity[:])
 
         warm_column = sb("warm_column", [P, 1], F32)
         nc.scalar.activation(warm_column[:], identity[:, 0:1], ACT.Sigmoid)
 
-        wg_raw = sb("wg_raw", [P, 2, H // 2], I32)
-        nc.sync.dma_start(wg_raw[:], wg_words.bitcast(I32).rearrange("a p w -> p a w"))
-        scale_rows = tab32[0, P * T :].rearrange("(a q r t) -> r q a t", a=2, q=4, r=4)
-        for r in range(4):
-            nc.sync.dma_start(tab_scales[r:P:PASS1_SHIFT, :], scale_rows[r])
-        tab_words = sb("tab_words", [P, T], I32, tag="after_word_gathers")
-        nc.sync.dma_start(tab_words[:], tab32[0, 0 : P * T].rearrange("(p t) -> p t", p=P))
-
-        wg_planes_raw = sb("wg_planes_raw", [P, 2, H // 4], I32, tag="after_wg_planes")
-        nc.vector.memset(wg_planes_raw[:], 0)
-        wg_scales32 = wg_scales.bitcast(I32)
-        for q in range(4):
-            nc.sync.dma_start(
-                wg_planes_raw[32 * q : 32 * q + 4, :, :],
-                wg_scales32[:, 4 * q : 4 * q + 4, :].rearrange("a r w -> r a w"),
-            )
-
-        nc.sync.dma_start(bias_rows[2:3].rearrange("o c p -> o (c p)"), bo.rearrange("(o n) -> o n", o=1))
-        plane1 = sb("plane1", [P, S // 4], I32)
-        nc.vector.memset(plane1[:], 0)
-
         nc.scalar.copy(
             bias_rows[0:2].rearrange("b t (ph el) -> b t ph el", el=4),
-            bg_rows[:].rearrange("b (ph t el) -> b t ph el", t=4, el=4),
+            bias_in[0:2].rearrange("b (ph t el) -> b t ph el", t=4, el=4),
         )
-        turned = wide_banks.tile([P, 4, P], F32, name="wide")
+        nc.scalar.copy(bias_rows[BO_ROW : BO_ROW + 1].rearrange("o c p -> o (c p)"), bias_in[BO_ROW : BO_ROW + 1])
+        turned = next_bank([P, 4, P])
         for t in range(4):
             nc.tensor.transpose(turned[:, t, :], bias_rows[:, t, :], identity[:])
-        bias_cols = sb("bias_cols", [P, 4, 3], F32)
-        nc.scalar.copy(bias_cols[:], turned[:, :, 0:3])
+        bias_cols = sb("bias_cols", [P, 4, BO_ROW + 1], F32)
+        nc.scalar.copy(bias_cols[:], turned[:, :, 0 : BO_ROW + 1])
 
-        plane0 = sb("plane0", [P, S], U8)
-        nc.vector.tensor_copy(plane0[:], tab_scales[:].bitcast(U8).indirect(offsets[:]))
-        nc.sync.dma_start(plane1[0 : P - PASS1_SHIFT, :], plane0[:].bitcast(I32)[PASS1_SHIFT:P, :])
-        picked_planes = [plane0[:], plane1[:].bitcast(U8)]
+        scale_rows = sb("scale_rows", [P, (S + H) // 4], I32)
+        nc.vector.tensor_copy(
+            scale_rows[0:SCALE_ROWS, S // 4 :].rearrange("p (b t ph) -> p b t ph", b=2, t=4),
+            wg_scale_rows[:].rearrange("p (b ph t) -> p b t ph", b=2, t=4),
+        )
+        picked_scales = placed("picked_scales", [P, S], U8, RAW - S // 2)
+        nc.vector.tensor_copy(picked_scales[:], tab_scales[:].bitcast(U8).indirect(offsets[:]))
+        nc.vector.tensor_copy(scale_rows[:, 0 : S // 4], picked_scales[:].bitcast(I32))
+        for q in range(4):
+            nc.sync.dma_start(planes[32 * q : 32 * q + 4], scale_rows[8 * q : 8 * q + 8, :])
+        picked_planes = [planes[:, a, 0 : S // 4].bitcast(U8) for a in range(2)]
 
         wv_raw, picked_codes, wg_codes = {}, [], []
 
-        def load_wv(b, a, raw):
+        def load_wv(b, a):
             rows, cols = slice(PASS * a, PASS * (a + 1)), slice(PASS * b, PASS * (b + 1))
-            nc.sync.dma_start(raw, wv[rows, cols].rearrange("(p i) c -> p i c", i=4))
-            wv_raw[b, a] = raw
+            wv_raw[b, a] = placed(f"wv_raw{b}{a}", [P, 4, PASS], F32, (2 * b + a) * RAW)
+            nc.sync.dma_start(wv_raw[b, a][:], wv[rows, cols].rearrange("(p i) c -> p i c", i=4))
 
-        def gather_words(half, tag):
-            picked = sb(f"picked{half}", [P, HALF], U32, tag=tag)
+        def gather_words(half):
+            picked = placed(f"picked{half}", [P, HALF], U32, 4 * RAW + 1024 * half)
             list_cols = slice(HALF // 16 * half, HALF // 16 * (half + 1))
             nc.vector.tensor_copy(picked[:], tab_words[:].bitcast(U32).indirect(offsets[:, list_cols]))
             parted = sb(f"parted{half}", [P, 2, 2 * HALF], U8)
@@ -109,49 +123,46 @@ def tile_list_gated_click_interests_kernel(tc, tab, offs, wv, wg_words, wg_scale
             picked_codes.append(parted)
 
         def permute_wg(b):
-            codes = sb(f"wg_codes{b}", [P, 2, 4, P // 2], I32, tag=f"after_gates{b}")
+            codes = sb(f"wg_codes{b}", [P, 2, 4, P // 2], I32)
             nc.vector.tensor_copy(
                 codes[:].rearrange("p a t (ph e) -> p a t ph e", e=2),
-                wg_raw[:, :, 256 * b : 256 * (b + 1)].rearrange("p a (ph t e) -> p a t ph e", t=4, e=2),
+                wg_raw[b][:].rearrange("p a (ph t e) -> p a t ph e", t=4, e=2),
             )
             wg_codes.append(codes)
 
+        load_wv(0, 0)
+        load_wv(0, 1)
+        gather_words(0)
         permute_wg(0)
-        permute_wg(1)
-        wv_first = sb("wv_first", [P, 2, 4, PASS], F32, tag="after_scale_gather")
-        load_wv(0, 0, wv_first[:, 0])
-        load_wv(0, 1, wv_first[:, 1])
-        gather_words(0, "after_first_parting")
 
-        warm_bank = wide_banks.tile([P, HALF], F32, name="wide")
+        warm_bank = next_bank([P, HALF])
         for t in range(WARM_PASSES):
             nc.tensor.matmul_mx(
                 out=warm_bank[:],
-                lhsT=wg_codes[0][:, 0, t, :].bitcast(FP4X4),
-                lhsT_scale=wg_planes_raw[:, 0, 0 : P // 4].bitcast(U8),
-                rhs=wg_raw[:, 0, 0 : HALF // 2].bitcast(FP4X4),
-                rhs_scale=wg_planes_raw[:, 0, 0 : HALF // 4].bitcast(U8),
+                lhsT=wg_raw[1][:, 0, 0 : P // 2].bitcast(FP4X4),
+                lhsT_scale=scale_rows[:, 0 : P // 4].bitcast(U8),
+                rhs=wg_raw[1][:, 1, :].bitcast(FP4X4),
+                rhs_scale=scale_rows[:, 0 : HALF // 4].bitcast(U8),
                 start=True,
                 stop=True,
             )
 
-        wg_planes = sb("wg_planes", [P, 4, 4, P // 4], I32, tag="after_first_parting")
-        nc.vector.tensor_copy(wg_planes[:], wg_planes_raw[:].rearrange("p a (b ph t) -> p (a b) t ph", b=2, t=4))
-        gather_words(1, "after_wg_planes")
-        load_wv(1, 0, sb("wv_raw10", [P, 4, PASS], F32, tag="after_word_gathers")[:])
-        load_wv(1, 1, sb("wv_raw11", [P, 4, PASS], F32, tag="after_wg_planes")[:])
+        gather_words(1)
+        permute_wg(1)
+        load_wv(1, 0)
+        load_wv(1, 1)
 
         gate = {}
 
         def gate_tile(b, half, t):
             if t == 0:
                 gate[b, half] = sb(f"gate{b}{half}", [P, 4, HALF], F32)
-            z = wide_banks.tile([P, HALF], F32, name="wide")
+            z = next_bank([P, HALF])
             for a in range(2):
                 nc.tensor.matmul_mx(
                     out=z[:],
                     lhsT=wg_codes[b][:, a, t, :].bitcast(FP4X4),
-                    lhsT_scale=wg_planes[:, 2 * a + b, t, :].bitcast(U8),
+                    lhsT_scale=planes[:, a, S // 4 + 32 * (4 * b + t) : S // 4 + 32 * (4 * b + t + 1)].bitcast(U8),
                     rhs=picked_codes[half][:, a, :].bitcast(FP4X4),
                     rhs_scale=picked_planes[a][:, HALF * half : HALF * (half + 1)],
                     start=(a == 0),
@@ -161,19 +172,19 @@ def tile_list_gated_click_interests_kernel(tc, tab, offs, wv, wg_words, wg_scale
 
         wv_bf, wv_codes, wv_planes = {}, {}, {}
 
-        def wv_rounding_views(b, a, tag):
-            wv_bf[b, a] = sb(f"wv_bf{b}{a}", [P, 4, PASS], BF16, tag=tag)
+        def wv_rounding_views(b, a):
+            wv_bf[b, a] = sb(f"wv_bf{b}{a}", [P, 4, PASS], BF16)
             return (
                 wv_bf[b, a][:].rearrange("p t (ph el i) -> p t ph i el", el=4, i=4),
-                wv_raw[b, a].rearrange("p i (ph t el) -> p t ph i el", t=4, el=4),
+                wv_raw[b, a][:].rearrange("p i (ph t el) -> p t ph i el", t=4, el=4),
             )
 
         def round_wv_on_vector(b, a):
-            dst, src = wv_rounding_views(b, a, f"after_quantise_wv{b}{a}")
+            dst, src = wv_rounding_views(b, a)
             nc.vector.tensor_copy(dst, src)
 
         def round_wv_on_scalar(b, a):
-            dst, src = wv_rounding_views(b, a, "after_gates0")
+            dst, src = wv_rounding_views(b, a)
             for t in range(4):
                 nc.scalar.copy(dst[:, t], src[:, t])
 
@@ -192,7 +203,7 @@ def tile_list_gated_click_interests_kernel(tc, tab, offs, wv, wg_words, wg_scale
 
         def value_chunk(b, chunk):
             half, j0 = divmod(chunk * CHUNK, HALF)
-            val = value_banks.tile([P, 4, CHUNK], F32, name="val")
+            val = next_bank([P, 4, CHUNK])
             for t in range(4):
                 for a in range(2):
                     nc.tensor.matmul_mx(
@@ -219,39 +230,46 @@ def tile_list_gated_click_interests_kernel(tc, tab, offs, wv, wg_words, wg_scale
 
         wo_raw, wo_bf, wo_codes, wo_planes = {}, {}, {}, {}
 
-        def load_wo(b, tag):
-            wo_raw[b] = sb(f"wo_raw{b}", [P, 4, N], F32, tag=tag)
+        def load_wo(b):
+            wo_raw[b] = placed(f"wo_raw{b}", [P, 4, N], F32, b * RAW)
             rows = wo[PASS * b : PASS * (b + 1), :].rearrange("(ph t el) n -> t ph el n", t=4, el=4)
             for t in range(4):
                 nc.sync.dma_start(wo_raw[b][:, t, :], rows[t])
 
-        def round_wo(b):
-            wo_bf[b] = sb(f"wo_bf{b}", [P, 4 * N], BF16)
-            for n0 in range(0, N, N // 2):
-                nc.scalar.copy(
-                    wo_bf[b][:, 4 * n0 : 4 * (n0 + N // 2)].rearrange("p (c u t) -> p c t u", u=4, t=4),
-                    wo_raw[b][:, :, n0 : n0 + N // 2].rearrange("p t (c u) -> p c t u", u=4),
+        def round_wo(b, side):
+            wo_bf[b, side] = sb(f"wo_bf{b}{side}", [P, 2 * N], BF16)
+            for n0 in range(0, N // 2, WO_STEP):
+                first = N // 2 * side + n0
+                nc.gpsimd.tensor_scalar(
+                    wo_bf[b, side][:, 4 * n0 : 4 * (n0 + WO_STEP)].rearrange("p (n t) -> p n t", t=4),
+                    wo_raw[b][:, :, first : first + WO_STEP].rearrange("p t n -> p n t"),
+                    1.0,
+                    0.0,
+                    ALU.mult,
+                    ALU.add,
                 )
 
-        def quantise_wo(b):
-            wo_codes[b] = sb(f"wo_codes{b}", [P, N], U32)
-            wo_planes[b] = sb(f"wo_planes{b}", [P, N], U8)
-            nc.vector.quantize_mx(out=wo_codes[b][:].bitcast(FP8X4), scales=wo_planes[b][:], in_=wo_bf[b][:])
+        def quantise_wo(b, side):
+            wo_codes[b, side] = sb(f"wo_codes{b}{side}", [P, N // 2], U32)
+            wo_planes[b, side] = sb(f"wo_planes{b}{side}", [P, N // 2], U8)
+            nc.vector.quantize_mx(
+                out=wo_codes[b, side][:].bitcast(FP8X4), scales=wo_planes[b, side][:], in_=wo_bf[b, side][:]
+            )
 
         out_rows = out.rearrange("(nt p) j -> p nt j", p=P)
 
         def out_piece(index):
             j0, width = PIECES[index]
             for nt0 in (0, 2):
-                acc = wide_banks.tile([P, 2, width], F32, name="wide")
+                acc = next_bank([P, 2, width])
                 res = sb(f"res{index}{nt0}", [P, 2, width], F32)
                 for slot in range(2):
-                    cols = slice(P * (nt0 + slot), P * (nt0 + slot + 1))
+                    cols = slice(P * slot, P * (slot + 1))
                     for b in range(2):
                         nc.tensor.matmul_mx(
                             out=acc[:, slot, :],
-                            lhsT=wo_codes[b][:, cols].bitcast(FP8X4),
-                            lhsT_scale=wo_planes[b][:, cols],
+                            lhsT=wo_codes[b, nt0 // 2][:, cols].bitcast(FP8X4),
+                            lhsT_scale=wo_planes[b, nt0 // 2][:, cols],
                             rhs=h_codes[b][:, j0 : j0 + width].bitcast(FP8X4),
                             rhs_scale=h_planes[b][:, j0 : j0 + width],
                             start=(b == 0),
@@ -259,47 +277,57 @@ def tile_list_gated_click_interests_kernel(tc, tab, offs, wv, wg_words, wg_scale
                         )
                 on_vector = index == len(PIECES) - 1 and nt0 == 0
                 for slot in range(2):
-                    bias = bias_cols[:, nt0 + slot, 2:3]
+                    bias = bias_cols[:, nt0 + slot, BO_ROW : BO_ROW + 1]
                     if on_vector:
                         nc.vector.tensor_scalar(res[:, slot, :], acc[:, slot, :], bias, None, ALU.add)
                     else:
                         nc.scalar.activation(res[:, slot, :], acc[:, slot, :], ACT.Identity, bias=bias)
                 nc.sync.dma_start(out_rows[:, nt0 : nt0 + 2, j0 : j0 + width], res[:])
 
-        for half in range(2):
-            for t in range(4):
-                gate_tile(0, half, t)
-        round_wv_on_vector(0, 0)
-        quantise_wv(0, 0)
-        round_wv_on_vector(0, 1)
-        load_wo(0, "after_scale_gather")
-        quantise_wv(0, 1)
-        load_wo(1, "after_quantise_wv01")
-        round_wv_on_vector(1, 0)
+        gates = [(b, half, t) for b in range(2) for half in range(2) for t in range(4)]
+        for b, half, t in gates[:EARLY_GATES]:
+            gate_tile(b, half, t)
+        for a in range(2):
+            round_wv_on_vector(0, a)
+            load_wo(a)
+            quantise_wv(0, a)
+        for a in range(2):
+            round_wv_on_scalar(1, a)
+        for b in range(2):
+            for side in range(2):
+                round_wo(b, side)
 
-        between_chunks = {0: (quantise_wv, 1, 0), 3: (round_wv_on_scalar, 1, 1), 5: (quantise_wv, 1, 1)}
         for chunk in range(CHUNKS):
-            gate_tile(1, chunk // 4, chunk % 4)
             value_chunk(0, chunk)
-            if chunk in between_chunks:
-                step, b, a = between_chunks[chunk]
-                step(b, a)
+            if chunk == 4:
+                quantise_wv(1, 0)
+            if chunk == 6:
+                quantise_wv(1, 1)
             if chunk > 0 and chunk % 2 == 0:
                 quantise_h(0, chunk - 2, 2)
-        for b in range(2):
-            round_wo(b)
+        for b, half, t in gates[EARLY_GATES:]:
+            gate_tile(b, half, t)
 
         value_chunk(1, 0)
-        quantise_wo(0)
+        quantise_wo(0, 0)
+        quantise_wo(0, 1)
         quantise_h(0, CHUNKS - 2, 2)
         value_chunk(1, 1)
-        quantise_wo(1)
-        for chunk in range(2, CHUNKS):
-            value_chunk(1, chunk)
-            if chunk % 2 == 0:
-                quantise_h(1, chunk - 2, 2)
-                out_piece(chunk // 2 - 1)
-        quantise_h(1, CHUNKS - 2, 1)
-        out_piece(len(PIECES) - 2)
-        quantise_h(1, CHUNKS - 1, 1)
-        out_piece(len(PIECES) - 1)
+        value_chunk(1, 2)
+        quantise_wo(1, 0)
+        quantise_h(1, 0, 2)
+        value_chunk(1, 3)
+        quantise_wo(1, 1)
+        value_chunk(1, 4)
+        quantise_h(1, 2, 2)
+        out_piece(0)
+        value_chunk(1, 5)
+        value_chunk(1, 6)
+        quantise_h(1, 4, 2)
+        out_piece(1)
+        value_chunk(1, 7)
+        quantise_h(1, 6, 1)
+        out_piece(2)
+        out_piece(3)
+        quantise_h(1, 7, 1)
+        out_piece(4)

@@ -25,10 +25,16 @@ CHUNKS = S // CHUNK
 PIECES = [(0, 256), (256, 256), (512, 256), (768, 128), (896, 128)]
 SCALE_ROWS = 32
 RAW = 4 * PASS * 4
+KIB = 1024
+AT_WG1 = 0
+AT_PICKED_SCALES = 3 * KIB // 2
+AT_WV0 = 2 * KIB
+AT_PICKED = AT_WV0 + 2 * RAW - KIB
+AT_WG0 = AT_PICKED + 2 * KIB
+AT_TABLE = AT_WG0 + 2 * KIB
 BANKS, BANK_BYTES = 8, 2048
 WARM_PASSES = 3
 EARLY_GATES = 11
-WO_STEP = 128
 BO_ROW = 32
 
 
@@ -61,12 +67,16 @@ def tile_list_gated_click_interests_kernel(tc, tab, offs, wv, wg_words, wg_scale
         )
         wg_scale_rows = sb("wg_scale_rows", [SCALE_ROWS, H // 4], I32)
         nc.sync.dma_start(wg_scale_rows[:], wg_scales.bitcast(I32).rearrange("a r w -> r a w"))
-        tab_words = placed("tab_words", [P, T], I32, 2 * RAW)
+        tab_words = placed("tab_words", [P, T], I32, AT_TABLE)
         nc.sync.dma_start(tab_words[:], tab32[0, 0 : P * T].rearrange("(p t) -> p t", p=P))
         wg32 = wg_words.bitcast(I32).rearrange("a p w -> p a w")
-        wg_raw = [placed("wg_raw0", [P, 2, 256], I32, 4 * RAW + 2048), sb("wg_raw1", [P, 2, 256], I32)]
-        for b in range(2):
+        wg_raw = []
+
+        def load_wg(b):
+            wg_raw.append(placed(f"wg_raw{b}", [P, 2, 256], I32, (AT_WG0, AT_WG1)[b]))
             nc.sync.dma_start(wg_raw[b][:], wg32[:, :, 256 * b : 256 * (b + 1)])
+
+        load_wg(0)
 
         nc.vector.memset(tab_scales[32:64, :], 0)
         nc.gpsimd.memset(tab_scales[64:P, :], 0)
@@ -100,22 +110,23 @@ def tile_list_gated_click_interests_kernel(tc, tab, offs, wv, wg_words, wg_scale
             scale_rows[0:SCALE_ROWS, S // 4 :].rearrange("p (b t ph) -> p b t ph", b=2, t=4),
             wg_scale_rows[:].rearrange("p (b ph t) -> p b t ph", b=2, t=4),
         )
-        picked_scales = placed("picked_scales", [P, S], U8, RAW - S // 2)
+        picked_scales = placed("picked_scales", [P, S], U8, AT_PICKED_SCALES)
         nc.vector.tensor_copy(picked_scales[:], tab_scales[:].bitcast(U8).indirect(offsets[:]))
         nc.vector.tensor_copy(scale_rows[:, 0 : S // 4], picked_scales[:].bitcast(I32))
         for q in range(4):
             nc.sync.dma_start(planes[32 * q : 32 * q + 4], scale_rows[8 * q : 8 * q + 8, :])
+        load_wg(1)
         picked_planes = [planes[:, a, 0 : S // 4].bitcast(U8) for a in range(2)]
 
         wv_raw, picked_codes, wg_codes = {}, [], []
 
         def load_wv(b, a):
             rows, cols = slice(PASS * a, PASS * (a + 1)), slice(PASS * b, PASS * (b + 1))
-            wv_raw[b, a] = placed(f"wv_raw{b}{a}", [P, 4, PASS], F32, (2 * b + a) * RAW)
+            wv_raw[b, a] = placed(f"wv_raw{b}{a}", [P, 4, PASS], F32, (AT_WV0, AT_TABLE)[b] + a * RAW)
             nc.sync.dma_start(wv_raw[b, a][:], wv[rows, cols].rearrange("(p i) c -> p i c", i=4))
 
         def gather_words(half):
-            picked = placed(f"picked{half}", [P, HALF], U32, 4 * RAW + 1024 * half)
+            picked = placed(f"picked{half}", [P, HALF], U32, AT_PICKED + KIB * half)
             list_cols = slice(HALF // 16 * half, HALF // 16 * (half + 1))
             nc.vector.tensor_copy(picked[:], tab_words[:].bitcast(U32).indirect(offsets[:, list_cols]))
             parted = sb(f"parted{half}", [P, 2, 2 * HALF], U8)
@@ -131,17 +142,17 @@ def tile_list_gated_click_interests_kernel(tc, tab, offs, wv, wg_words, wg_scale
             wg_codes.append(codes)
 
         load_wv(0, 0)
-        load_wv(0, 1)
         gather_words(0)
+        load_wv(0, 1)
         permute_wg(0)
 
         warm_bank = next_bank([P, HALF])
         for t in range(WARM_PASSES):
             nc.tensor.matmul_mx(
                 out=warm_bank[:],
-                lhsT=wg_raw[1][:, 0, 0 : P // 2].bitcast(FP4X4),
+                lhsT=tab_words[:, 0 : P // 2].bitcast(FP4X4),
                 lhsT_scale=scale_rows[:, 0 : P // 4].bitcast(U8),
-                rhs=wg_raw[1][:, 1, :].bitcast(FP4X4),
+                rhs=tab_words[:, 0 : HALF // 2].bitcast(FP4X4),
                 rhs_scale=scale_rows[:, 0 : HALF // 4].bitcast(U8),
                 start=True,
                 stop=True,
@@ -231,23 +242,17 @@ def tile_list_gated_click_interests_kernel(tc, tab, offs, wv, wg_words, wg_scale
         wo_raw, wo_bf, wo_codes, wo_planes = {}, {}, {}, {}
 
         def load_wo(b):
-            wo_raw[b] = placed(f"wo_raw{b}", [P, 4, N], F32, b * RAW)
+            wo_raw[b] = placed(f"wo_raw{b}", [P, 4, N], F32, AT_WV0 + b * RAW)
             rows = wo[PASS * b : PASS * (b + 1), :].rearrange("(ph t el) n -> t ph el n", t=4, el=4)
             for t in range(4):
                 nc.sync.dma_start(wo_raw[b][:, t, :], rows[t])
 
         def round_wo(b, side):
             wo_bf[b, side] = sb(f"wo_bf{b}{side}", [P, 2 * N], BF16)
-            for n0 in range(0, N // 2, WO_STEP):
-                first = N // 2 * side + n0
-                nc.gpsimd.tensor_scalar(
-                    wo_bf[b, side][:, 4 * n0 : 4 * (n0 + WO_STEP)].rearrange("p (n t) -> p n t", t=4),
-                    wo_raw[b][:, :, first : first + WO_STEP].rearrange("p t n -> p n t"),
-                    1.0,
-                    0.0,
-                    ALU.mult,
-                    ALU.add,
-                )
+            nc.scalar.copy(
+                wo_bf[b, side][:].rearrange("p (c u t) -> p c t u", u=4, t=4),
+                wo_raw[b][:, :, N // 2 * side : N // 2 * (side + 1)].rearrange("p t (c u) -> p c t u", u=4),
+            )
 
         def quantise_wo(b, side):
             wo_codes[b, side] = sb(f"wo_codes{b}{side}", [P, N // 2], U32)
@@ -291,21 +296,24 @@ def tile_list_gated_click_interests_kernel(tc, tab, offs, wv, wg_words, wg_scale
             round_wv_on_vector(0, a)
             load_wo(a)
             quantise_wv(0, a)
-        for a in range(2):
-            round_wv_on_scalar(1, a)
-        for b in range(2):
-            for side in range(2):
-                round_wo(b, side)
+        round_wv_on_scalar(1, 0)
+        for side in range(2):
+            round_wo(0, side)
 
         for chunk in range(CHUNKS):
             value_chunk(0, chunk)
+            if chunk == 2:
+                round_wv_on_vector(1, 1)
             if chunk == 4:
-                quantise_wv(1, 0)
-            if chunk == 6:
                 quantise_wv(1, 1)
+            if chunk == 5:
+                quantise_wv(1, 0)
             if chunk > 0 and chunk % 2 == 0:
                 quantise_h(0, chunk - 2, 2)
-        for b, half, t in gates[EARLY_GATES:]:
+        gate_tile(*gates[EARLY_GATES])
+        for side in range(2):
+            round_wo(1, side)
+        for b, half, t in gates[EARLY_GATES + 1 :]:
             gate_tile(b, half, t)
 
         value_chunk(1, 0)

@@ -29,12 +29,13 @@ KIB = 1024
 AT_WG1 = 0
 AT_PICKED_SCALES = 3 * KIB // 2
 AT_WV0 = 2 * KIB
-AT_PICKED = AT_WV0 + 2 * RAW - KIB
+AT_SCALE_ROWS = AT_WV0 + 2 * RAW - KIB
+AT_PICKED = AT_SCALE_ROWS + 2 * KIB
 AT_WG0 = AT_PICKED + 2 * KIB
 AT_TABLE = AT_WG0 + 2 * KIB
 BANKS, BANK_BYTES = 8, 2048
-WARM_PASSES = 3
-EARLY_GATES = 11
+WARM_PASSES = (3, 3)
+EARLY_GATES = 12
 BO_ROW = 32
 
 
@@ -44,12 +45,15 @@ def tile_list_gated_click_interests_kernel(tc, tab, offs, wv, wg_words, wg_scale
         keep = ctx.enter_context(tc.tile_pool(name="keep", bufs=1))
         turns = ctx.enter_context(tc.tile_pool(name="turns", bufs=1))
         psum = ctx.enter_context(tc.psum_pool(name="psum", bufs=1))
+
         banks_taken = []
 
-        def next_bank(shape):
-            turn = len(banks_taken)
-            banks_taken.append(turn)
-            return psum.tile(shape, F32, name=f"sums{turn}", offset=BANK_BYTES * (turn % BANKS))
+        def bank_tile(bank, shape):
+            banks_taken.append(bank)
+            return psum.tile(shape, F32, name=f"sums{len(banks_taken)}", offset=BANK_BYTES * bank)
+
+        def last_bank(name, shape):
+            return psum.tile(shape, F32, name=name, offset=BANK_BYTES * (BANKS - 1))
 
         def sb(name, shape, dt, tag=None):
             return keep.tile(shape, dt, name=name, tag=tag or name, align_bytes=64)
@@ -99,13 +103,13 @@ def tile_list_gated_click_interests_kernel(tc, tab, offs, wv, wg_words, wg_scale
             bias_in[0:2].rearrange("b (ph t el) -> b t ph el", t=4, el=4),
         )
         nc.scalar.copy(bias_rows[BO_ROW : BO_ROW + 1].rearrange("o c p -> o (c p)"), bias_in[BO_ROW : BO_ROW + 1])
-        turned = next_bank([P, 4, P])
+        turned = last_bank("turned", [P, 4, P])
         for t in range(4):
             nc.tensor.transpose(turned[:, t, :], bias_rows[:, t, :], identity[:])
         bias_cols = sb("bias_cols", [P, 4, BO_ROW + 1], F32)
         nc.scalar.copy(bias_cols[:], turned[:, :, 0 : BO_ROW + 1])
 
-        scale_rows = sb("scale_rows", [P, (S + H) // 4], I32)
+        scale_rows = placed("scale_rows", [P, (S + H) // 4], I32, AT_SCALE_ROWS)
         nc.vector.tensor_copy(
             scale_rows[0:SCALE_ROWS, S // 4 :].rearrange("p (b t ph) -> p b t ph", b=2, t=4),
             wg_scale_rows[:].rearrange("p (b ph t) -> p b t ph", b=2, t=4),
@@ -142,18 +146,18 @@ def tile_list_gated_click_interests_kernel(tc, tab, offs, wv, wg_words, wg_scale
             wg_codes.append(codes)
 
         load_wv(0, 0)
-        gather_words(0)
         load_wv(0, 1)
+        gather_words(0)
         permute_wg(0)
 
-        warm_bank = next_bank([P, HALF])
-        for t in range(WARM_PASSES):
+        warm_bank = last_bank("warm_bank", [P, HALF])
+        for words in [scale_rows] * WARM_PASSES[0] + [tab_words] * WARM_PASSES[1]:
             nc.tensor.matmul_mx(
                 out=warm_bank[:],
-                lhsT=tab_words[:, 0 : P // 2].bitcast(FP4X4),
-                lhsT_scale=scale_rows[:, 0 : P // 4].bitcast(U8),
-                rhs=tab_words[:, 0 : HALF // 2].bitcast(FP4X4),
-                rhs_scale=scale_rows[:, 0 : HALF // 4].bitcast(U8),
+                lhsT=words[:, 0 : P // 2].bitcast(FP4X4),
+                lhsT_scale=tab_scales[:, 0 : P // 4].bitcast(U8),
+                rhs=words[:, 0 : HALF // 2].bitcast(FP4X4),
+                rhs_scale=tab_scales[:, 0 : HALF // 4].bitcast(U8),
                 start=True,
                 stop=True,
             )
@@ -167,8 +171,10 @@ def tile_list_gated_click_interests_kernel(tc, tab, offs, wv, wg_words, wg_scale
 
         def gate_tile(b, half, t):
             if t == 0:
-                gate[b, half] = sb(f"gate{b}{half}", [P, 4, HALF], F32)
-            z = next_bank([P, HALF])
+                name, shape = f"gate{b}{half}", [P, 4, HALF]
+                last = (b, half) == (1, 1)
+                gate[b, half] = placed(name, shape, F32, AT_WV0 + RAW) if last else sb(name, shape, F32)
+            z = bank_tile((8 * b + 4 * half + t) % BANKS, [P, HALF])
             for a in range(2):
                 nc.tensor.matmul_mx(
                     out=z[:],
@@ -183,21 +189,13 @@ def tile_list_gated_click_interests_kernel(tc, tab, offs, wv, wg_words, wg_scale
 
         wv_bf, wv_codes, wv_planes = {}, {}, {}
 
-        def wv_rounding_views(b, a):
-            wv_bf[b, a] = sb(f"wv_bf{b}{a}", [P, 4, PASS], BF16)
-            return (
-                wv_bf[b, a][:].rearrange("p t (ph el i) -> p t ph i el", el=4, i=4),
-                wv_raw[b, a][:].rearrange("p i (ph t el) -> p t ph i el", t=4, el=4),
+        def round_wv(b, a, copy, slots):
+            if (b, a) not in wv_bf:
+                wv_bf[b, a] = sb(f"wv_bf{b}{a}", [P, 4, PASS], BF16)
+            copy(
+                wv_bf[b, a][:].rearrange("p t (ph el i) -> p t ph i el", el=4, i=4)[:, slots],
+                wv_raw[b, a][:].rearrange("p i (ph t el) -> p t ph i el", t=4, el=4)[:, slots],
             )
-
-        def round_wv_on_vector(b, a):
-            dst, src = wv_rounding_views(b, a)
-            nc.vector.tensor_copy(dst, src)
-
-        def round_wv_on_scalar(b, a):
-            dst, src = wv_rounding_views(b, a)
-            for t in range(4):
-                nc.scalar.copy(dst[:, t], src[:, t])
 
         def quantise_wv(b, a):
             wv_codes[b, a] = sb(f"wv_codes{b}{a}", [P, PASS], U32)
@@ -214,7 +212,7 @@ def tile_list_gated_click_interests_kernel(tc, tab, offs, wv, wg_words, wg_scale
 
         def value_chunk(b, chunk):
             half, j0 = divmod(chunk * CHUNK, HALF)
-            val = next_bank([P, 4, CHUNK])
+            val = bank_tile((chunk + 4) % BANKS if b == 0 else chunk % 4, [P, 4, CHUNK])
             for t in range(4):
                 for a in range(2):
                     nc.tensor.matmul_mx(
@@ -247,38 +245,36 @@ def tile_list_gated_click_interests_kernel(tc, tab, offs, wv, wg_words, wg_scale
             for t in range(4):
                 nc.sync.dma_start(wo_raw[b][:, t, :], rows[t])
 
-        def round_wo(b, side):
-            wo_bf[b, side] = sb(f"wo_bf{b}{side}", [P, 2 * N], BF16)
+        def round_wo(b):
+            wo_bf[b] = sb(f"wo_bf{b}", [P, 4 * N], BF16)
             nc.scalar.copy(
-                wo_bf[b, side][:].rearrange("p (c u t) -> p c t u", u=4, t=4),
-                wo_raw[b][:, :, N // 2 * side : N // 2 * (side + 1)].rearrange("p t (c u) -> p c t u", u=4),
+                wo_bf[b][:].rearrange("p (c u t) -> p c t u", u=4, t=4),
+                wo_raw[b][:].rearrange("p t (c u) -> p c t u", u=4),
             )
 
-        def quantise_wo(b, side):
-            wo_codes[b, side] = sb(f"wo_codes{b}{side}", [P, N // 2], U32)
-            wo_planes[b, side] = sb(f"wo_planes{b}{side}", [P, N // 2], U8)
-            nc.vector.quantize_mx(
-                out=wo_codes[b, side][:].bitcast(FP8X4), scales=wo_planes[b, side][:], in_=wo_bf[b, side][:]
-            )
+        def quantise_wo(b):
+            wo_codes[b] = sb(f"wo_codes{b}", [P, N], U32)
+            wo_planes[b] = sb(f"wo_planes{b}", [P, N], U8)
+            nc.vector.quantize_mx(out=wo_codes[b][:].bitcast(FP8X4), scales=wo_planes[b][:], in_=wo_bf[b][:])
 
         out_rows = out.rearrange("(nt p) j -> p nt j", p=P)
 
         def out_piece(index):
             j0, width = PIECES[index]
             for nt0 in (0, 2):
-                acc = next_bank([P, 2, width])
+                acc = bank_tile(4 + (2 * index + nt0 // 2) % 4, [P, 2, width])
                 res = sb(f"res{index}{nt0}", [P, 2, width], F32)
                 for slot in range(2):
-                    cols = slice(P * slot, P * (slot + 1))
-                    for b in range(2):
+                    cols = slice(P * (nt0 + slot), P * (nt0 + slot + 1))
+                    for b in (1, 0):
                         nc.tensor.matmul_mx(
                             out=acc[:, slot, :],
-                            lhsT=wo_codes[b, nt0 // 2][:, cols].bitcast(FP8X4),
-                            lhsT_scale=wo_planes[b, nt0 // 2][:, cols],
+                            lhsT=wo_codes[b][:, cols].bitcast(FP8X4),
+                            lhsT_scale=wo_planes[b][:, cols],
                             rhs=h_codes[b][:, j0 : j0 + width].bitcast(FP8X4),
                             rhs_scale=h_planes[b][:, j0 : j0 + width],
-                            start=(b == 0),
-                            stop=(b == 1),
+                            start=(b == 1),
+                            stop=(b == 0),
                         )
                 on_vector = index == len(PIECES) - 1 and nt0 == 0
                 for slot in range(2):
@@ -293,49 +289,46 @@ def tile_list_gated_click_interests_kernel(tc, tab, offs, wv, wg_words, wg_scale
         for b, half, t in gates[:EARLY_GATES]:
             gate_tile(b, half, t)
         for a in range(2):
-            round_wv_on_vector(0, a)
+            round_wv(0, a, nc.vector.tensor_copy, slice(0, 4))
             load_wo(a)
             quantise_wv(0, a)
-        round_wv_on_scalar(1, 0)
-        for side in range(2):
-            round_wo(0, side)
+        round_wv(1, 0, nc.vector.tensor_copy, slice(0, 2))
+        round_wv(1, 0, nc.scalar.copy, slice(2, 4))
+        round_wv(1, 1, nc.scalar.copy, slice(0, 4))
+        for b in range(2):
+            round_wo(b)
 
         for chunk in range(CHUNKS):
             value_chunk(0, chunk)
-            if chunk == 2:
-                round_wv_on_vector(1, 1)
+            if chunk == 1:
+                quantise_wv(1, 0)
             if chunk == 4:
                 quantise_wv(1, 1)
             if chunk == 5:
-                quantise_wv(1, 0)
-            if chunk > 0 and chunk % 2 == 0:
-                quantise_h(0, chunk - 2, 2)
-        gate_tile(*gates[EARLY_GATES])
-        for side in range(2):
-            round_wo(1, side)
-        for b, half, t in gates[EARLY_GATES + 1 :]:
+                quantise_h(0, 0, 4)
+            if chunk == 7:
+                quantise_wo(0)
+        for b, half, t in gates[EARLY_GATES:]:
             gate_tile(b, half, t)
 
         value_chunk(1, 0)
-        quantise_wo(0, 0)
-        quantise_wo(0, 1)
-        quantise_h(0, CHUNKS - 2, 2)
         value_chunk(1, 1)
-        value_chunk(1, 2)
-        quantise_wo(1, 0)
+        quantise_wo(1)
         quantise_h(1, 0, 2)
+        value_chunk(1, 2)
         value_chunk(1, 3)
-        quantise_wo(1, 1)
-        value_chunk(1, 4)
-        quantise_h(1, 2, 2)
         out_piece(0)
+        quantise_h(0, 4, 2)
+        quantise_h(1, 2, 2)
+        value_chunk(1, 4)
         value_chunk(1, 5)
-        value_chunk(1, 6)
-        quantise_h(1, 4, 2)
         out_piece(1)
+        quantise_h(0, 6, 2)
+        quantise_h(1, 4, 2)
+        value_chunk(1, 6)
         value_chunk(1, 7)
-        quantise_h(1, 6, 1)
         out_piece(2)
+        quantise_h(1, 6, 1)
         out_piece(3)
         quantise_h(1, 7, 1)
         out_piece(4)

@@ -82,6 +82,8 @@ def tile_list_gated_click_interests_kernel(tc, tab, offs, wv, wg_words, wg_scale
 
         load_wg(0)
 
+        warm_zero = sb("warm_zero", [P, 1], F32)
+        nc.gpsimd.memset(warm_zero[:], 0.0)
         nc.vector.memset(tab_scales[32:64, :], 0)
         nc.gpsimd.memset(tab_scales[64:P, :], 0)
         planes = sb("planes", [P, 2, (S + H) // 4], I32)
@@ -96,7 +98,7 @@ def tile_list_gated_click_interests_kernel(tc, tab, offs, wv, wg_words, wg_scale
         make_identity(nc, identity[:])
 
         warm_column = sb("warm_column", [P, 1], F32)
-        nc.scalar.activation(warm_column[:], identity[:, 0:1], ACT.Sigmoid)
+        nc.scalar.activation(warm_column[:], warm_zero[:], ACT.Sigmoid)
 
         nc.scalar.copy(
             bias_rows[0:2].rearrange("b t (ph el) -> b t ph el", el=4),
@@ -119,7 +121,6 @@ def tile_list_gated_click_interests_kernel(tc, tab, offs, wv, wg_words, wg_scale
         nc.vector.tensor_copy(scale_rows[:, 0 : S // 4], picked_scales[:].bitcast(I32))
         for q in range(4):
             nc.sync.dma_start(planes[32 * q : 32 * q + 4], scale_rows[8 * q : 8 * q + 8, :])
-        load_wg(1)
         picked_planes = [planes[:, a, 0 : S // 4].bitcast(U8) for a in range(2)]
 
         wv_raw, picked_codes, wg_codes = {}, [], []
@@ -146,6 +147,7 @@ def tile_list_gated_click_interests_kernel(tc, tab, offs, wv, wg_words, wg_scale
             wg_codes.append(codes)
 
         load_wv(0, 0)
+        load_wg(1)
         load_wv(0, 1)
         gather_words(0)
         permute_wg(0)
@@ -163,7 +165,6 @@ def tile_list_gated_click_interests_kernel(tc, tab, offs, wv, wg_words, wg_scale
             )
 
         gather_words(1)
-        permute_wg(1)
         load_wv(1, 0)
         load_wv(1, 1)
 
@@ -191,7 +192,8 @@ def tile_list_gated_click_interests_kernel(tc, tab, offs, wv, wg_words, wg_scale
 
         def round_wv(b, a, copy, slots):
             if (b, a) not in wv_bf:
-                wv_bf[b, a] = sb(f"wv_bf{b}{a}", [P, 4, PASS], BF16)
+                tag = "second_rounded" if a != b else None
+                wv_bf[b, a] = sb(f"wv_bf{b}{a}", [P, 4, PASS], BF16, tag=tag)
             copy(
                 wv_bf[b, a][:].rearrange("p t (ph el i) -> p t ph i el", el=4, i=4)[:, slots],
                 wv_raw[b, a][:].rearrange("p i (ph t el) -> p t ph i el", t=4, el=4)[:, slots],
@@ -214,15 +216,15 @@ def tile_list_gated_click_interests_kernel(tc, tab, offs, wv, wg_words, wg_scale
             half, j0 = divmod(chunk * CHUNK, HALF)
             val = bank_tile((chunk + 4) % BANKS if b == 0 else chunk % 4, [P, 4, CHUNK])
             for t in range(4):
-                for a in range(2):
+                for a in (1, 0):
                     nc.tensor.matmul_mx(
                         out=val[:, t, :],
                         lhsT=wv_codes[b, a][:, P * t : P * (t + 1)].bitcast(FP8X4),
                         lhsT_scale=wv_planes[b, a][:, P * t : P * (t + 1)],
                         rhs=picked_codes[half][:, a, 2 * j0 : 2 * (j0 + CHUNK)].bitcast(FP4X4),
                         rhs_scale=picked_planes[a][:, chunk * CHUNK : (chunk + 1) * CHUNK],
-                        start=(a == 0),
-                        stop=(a == 1),
+                        start=(a == 1),
+                        stop=(a == 0),
                     )
             nc.vector.tensor_tensor(
                 h_bf[b][:, 4 * CHUNK * chunk : 4 * CHUNK * (chunk + 1)].rearrange("p (c u t) -> p c t u", u=4, t=4),
@@ -286,12 +288,17 @@ def tile_list_gated_click_interests_kernel(tc, tab, offs, wv, wg_words, wg_scale
                 nc.sync.dma_start(out_rows[:, nt0 : nt0 + 2, j0 : j0 + width], res[:])
 
         gates = [(b, half, t) for b in range(2) for half in range(2) for t in range(4)]
-        for b, half, t in gates[:EARLY_GATES]:
+        for b, half, t in gates[:8]:
             gate_tile(b, half, t)
-        for a in range(2):
-            round_wv(0, a, nc.vector.tensor_copy, slice(0, 4))
-            load_wo(a)
-            quantise_wv(0, a)
+        round_wv(0, 0, nc.vector.tensor_copy, slice(0, 4))
+        load_wo(0)
+        permute_wg(1)
+        quantise_wv(0, 0)
+        round_wv(0, 1, nc.vector.tensor_copy, slice(0, 4))
+        load_wo(1)
+        quantise_wv(0, 1)
+        for b, half, t in gates[8:EARLY_GATES]:
+            gate_tile(b, half, t)
         round_wv(1, 0, nc.vector.tensor_copy, slice(0, 2))
         round_wv(1, 0, nc.scalar.copy, slice(2, 4))
         round_wv(1, 1, nc.scalar.copy, slice(0, 4))

@@ -299,8 +299,7 @@ def tile_list_gated_click_interests_kernel(tc, tab, offs, wv, wg_words, wg_scale
         quantise_wv(0, 1)
         for b, half, t in gates[8:EARLY_GATES]:
             gate_tile(b, half, t)
-        round_wv(1, 0, nc.vector.tensor_copy, slice(0, 2))
-        round_wv(1, 0, nc.scalar.copy, slice(2, 4))
+        round_wv(1, 0, nc.vector.tensor_copy, slice(0, 4))
         round_wv(1, 1, nc.scalar.copy, slice(0, 4))
         for b in range(2):
             round_wo(b)

@@ -25,14 +25,16 @@ CHUNKS = S // CHUNK
 PIECES = [(0, 256), (256, 256), (512, 256), (768, 128), (896, 128)]
 SCALE_ROWS = 32
 RAW = 4 * PASS * 4
+PART = HALF // 4
 KIB = 1024
 AT_WG1 = 0
 AT_PICKED_SCALES = 3 * KIB // 2
 AT_WV0 = 2 * KIB
 AT_SCALE_ROWS = AT_WV0 + 2 * RAW - KIB
-AT_PICKED = AT_SCALE_ROWS + 2 * KIB
-AT_WG0 = AT_PICKED + 2 * KIB
-AT_TABLE = AT_WG0 + 2 * KIB
+AT_WG0 = AT_SCALE_ROWS + 2 * KIB
+AT_PICKED1 = AT_WG0 + KIB
+AT_TABLE = AT_PICKED1 + 2 * KIB
+AT_ROUNDED = AT_TABLE + 2 * RAW
 BANKS, BANK_BYTES = 8, 2048
 WARM_PASSES = (3, 3)
 EARLY_GATES = 12
@@ -86,7 +88,7 @@ def tile_list_gated_click_interests_kernel(tc, tab, offs, wv, wg_words, wg_scale
         nc.gpsimd.memset(warm_zero[:], 0.0)
         nc.vector.memset(tab_scales[32:64, :], 0)
         nc.gpsimd.memset(tab_scales[64:P, :], 0)
-        planes = sb("planes", [P, 2, (S + H) // 4], I32)
+        planes = sb("planes", [P, 2, 2, 2 * PART], I32)
         nc.vector.memset(planes[:], 0)
 
         bias_in = sb("bias_in", [BO_ROW + 1, PASS], F32)
@@ -111,19 +113,27 @@ def tile_list_gated_click_interests_kernel(tc, tab, offs, wv, wg_words, wg_scale
         bias_cols = sb("bias_cols", [P, 4, BO_ROW + 1], F32)
         nc.scalar.copy(bias_cols[:], turned[:, :, 0 : BO_ROW + 1])
 
-        scale_rows = placed("scale_rows", [P, (S + H) // 4], I32, AT_SCALE_ROWS)
-        nc.vector.tensor_copy(
-            scale_rows[0:SCALE_ROWS, S // 4 :].rearrange("p (b t ph) -> p b t ph", b=2, t=4),
-            wg_scale_rows[:].rearrange("p (b ph t) -> p b t ph", b=2, t=4),
-        )
+        scale_rows = [
+            placed("scale_rows0", [P, 2 * PART], I32, AT_SCALE_ROWS),
+            sb("scale_rows1", [P, 2 * PART], I32),
+        ]
+        for b in range(2):
+            nc.vector.tensor_copy(
+                scale_rows[b][0:SCALE_ROWS, PART:].rearrange("p (t ph) -> p t ph", t=4),
+                wg_scale_rows[:, PART * b : PART * (b + 1)].rearrange("p (ph t) -> p t ph", t=4),
+            )
         picked_scales = placed("picked_scales", [P, S], U8, AT_PICKED_SCALES)
         nc.vector.tensor_copy(picked_scales[:], tab_scales[:].bitcast(U8).indirect(offsets[:]))
-        nc.vector.tensor_copy(scale_rows[:, 0 : S // 4], picked_scales[:].bitcast(I32))
-        for q in range(4):
-            nc.sync.dma_start(planes[32 * q : 32 * q + 4], scale_rows[8 * q : 8 * q + 8, :])
-        picked_planes = [planes[:, a, 0 : S // 4].bitcast(U8) for a in range(2)]
+        for half in range(2):
+            nc.vector.tensor_copy(
+                scale_rows[half][:, 0:PART], picked_scales[:].bitcast(I32)[:, PART * half : PART * (half + 1)]
+            )
 
-        wv_raw, picked_codes, wg_codes = {}, [], []
+        def move_planes(part):
+            for q in range(4):
+                nc.sync.dma_start(planes[32 * q : 32 * q + 4, part], scale_rows[part][8 * q : 8 * q + 8, :])
+
+        wv_raw, picked_words, picked_codes, wg_codes = {}, [], [], []
 
         def load_wv(b, a):
             rows, cols = slice(PASS * a, PASS * (a + 1)), slice(PASS * b, PASS * (b + 1))
@@ -131,12 +141,15 @@ def tile_list_gated_click_interests_kernel(tc, tab, offs, wv, wg_words, wg_scale
             nc.sync.dma_start(wv_raw[b, a][:], wv[rows, cols].rearrange("(p i) c -> p i c", i=4))
 
         def gather_words(half):
-            picked = placed(f"picked{half}", [P, HALF], U32, AT_PICKED + KIB * half)
+            name, shape = f"picked{half}", [P, HALF]
+            picked = sb(name, shape, U32) if half == 0 else placed(name, shape, U32, AT_PICKED1)
             list_cols = slice(HALF // 16 * half, HALF // 16 * (half + 1))
             nc.vector.tensor_copy(picked[:], tab_words[:].bitcast(U32).indirect(offsets[:, list_cols]))
-            parted = sb(f"parted{half}", [P, 2, 2 * HALF], U8)
-            nc.vector.tensor_copy(parted[:].bitcast(U16), picked[:].bitcast(U16).rearrange("p (j a) -> p a j", a=2))
-            picked_codes.append(parted)
+            picked_words.append(picked[:].bitcast(U16).rearrange("p (j a) -> p a j", a=2))
+            picked_codes.append(sb(f"parted{half}", [P, 2, 2 * HALF], U8))
+
+        def part_words(half, passes):
+            nc.vector.tensor_copy(picked_codes[half][:].bitcast(U16)[:, passes], picked_words[half][:, passes])
 
         def permute_wg(b):
             codes = sb(f"wg_codes{b}", [P, 2, 4, P // 2], I32)
@@ -146,25 +159,30 @@ def tile_list_gated_click_interests_kernel(tc, tab, offs, wv, wg_words, wg_scale
             )
             wg_codes.append(codes)
 
+        move_planes(0)
         load_wv(0, 0)
+        move_planes(1)
         load_wg(1)
         load_wv(0, 1)
         gather_words(0)
         permute_wg(0)
+        part_words(0, slice(0, 1))
+        part_words(0, slice(1, 2))
 
         warm_bank = last_bank("warm_bank", [P, HALF])
-        for words in [scale_rows] * WARM_PASSES[0] + [tab_words] * WARM_PASSES[1]:
+        for words in [scale_rows[1]] * WARM_PASSES[0] + [tab_words] * WARM_PASSES[1]:
             nc.tensor.matmul_mx(
                 out=warm_bank[:],
                 lhsT=words[:, 0 : P // 2].bitcast(FP4X4),
                 lhsT_scale=tab_scales[:, 0 : P // 4].bitcast(U8),
-                rhs=words[:, 0 : HALF // 2].bitcast(FP4X4),
+                rhs=tab_scales[:, 0 : HALF // 2].bitcast(FP4X4),
                 rhs_scale=tab_scales[:, 0 : HALF // 4].bitcast(U8),
                 start=True,
                 stop=True,
             )
 
         gather_words(1)
+        part_words(1, slice(0, 2))
         load_wv(1, 0)
         load_wv(1, 1)
 
@@ -180,9 +198,9 @@ def tile_list_gated_click_interests_kernel(tc, tab, offs, wv, wg_words, wg_scale
                 nc.tensor.matmul_mx(
                     out=z[:],
                     lhsT=wg_codes[b][:, a, t, :].bitcast(FP4X4),
-                    lhsT_scale=planes[:, a, S // 4 + 32 * (4 * b + t) : S // 4 + 32 * (4 * b + t + 1)].bitcast(U8),
+                    lhsT_scale=planes[:, b, a, PART + 32 * t : PART + 32 * (t + 1)].bitcast(U8),
                     rhs=picked_codes[half][:, a, :].bitcast(FP4X4),
-                    rhs_scale=picked_planes[a][:, HALF * half : HALF * (half + 1)],
+                    rhs_scale=planes[:, half, a, 0:PART].bitcast(U8),
                     start=(a == 0),
                     stop=(a == 1),
                 )
@@ -190,22 +208,23 @@ def tile_list_gated_click_interests_kernel(tc, tab, offs, wv, wg_words, wg_scale
 
         wv_bf, wv_codes, wv_planes = {}, {}, {}
 
-        def round_wv(b, a, copy, slots):
-            if (b, a) not in wv_bf:
-                tag = "second_rounded" if a != b else None
-                wv_bf[b, a] = sb(f"wv_bf{b}{a}", [P, 4, PASS], BF16, tag=tag)
+        def round_wv(b, a, copy, first, slots, at=None):
+            name, shape = f"wv_bf{b}{a}{first}", [P, slots, PASS]
+            wv_bf[b, a, first] = sb(name, shape, BF16) if at is None else placed(name, shape, BF16, at)
             copy(
-                wv_bf[b, a][:].rearrange("p t (ph el i) -> p t ph i el", el=4, i=4)[:, slots],
-                wv_raw[b, a][:].rearrange("p i (ph t el) -> p t ph i el", t=4, el=4)[:, slots],
+                wv_bf[b, a, first][:].rearrange("p t (ph el i) -> p t ph i el", el=4, i=4),
+                wv_raw[b, a][:].rearrange("p i (ph t el) -> p t ph i el", t=4, el=4)[:, first : first + slots],
             )
 
-        def quantise_wv(b, a):
-            wv_codes[b, a] = sb(f"wv_codes{b}{a}", [P, PASS], U32)
-            wv_planes[b, a] = sb(f"wv_planes{b}{a}", [P, PASS], U8)
+        def quantise_wv(b, a, first, slots):
+            if first == 0:
+                wv_codes[b, a] = sb(f"wv_codes{b}{a}", [P, PASS], U32)
+                wv_planes[b, a] = sb(f"wv_planes{b}{a}", [P, PASS], U8)
+            cols = slice(P * first, P * (first + slots))
             nc.vector.quantize_mx(
-                out=wv_codes[b, a][:].bitcast(FP8X4),
-                scales=wv_planes[b, a][:],
-                in_=wv_bf[b, a][:].rearrange("p t c -> p (t c)"),
+                out=wv_codes[b, a][:, cols].bitcast(FP8X4),
+                scales=wv_planes[b, a][:, cols],
+                in_=wv_bf[b, a, first][:].rearrange("p t c -> p (t c)"),
             )
 
         h_bf = [sb(f"h_bf{b}", [P, 4 * S], BF16) for b in range(2)]
@@ -222,7 +241,7 @@ def tile_list_gated_click_interests_kernel(tc, tab, offs, wv, wg_words, wg_scale
                         lhsT=wv_codes[b, a][:, P * t : P * (t + 1)].bitcast(FP8X4),
                         lhsT_scale=wv_planes[b, a][:, P * t : P * (t + 1)],
                         rhs=picked_codes[half][:, a, 2 * j0 : 2 * (j0 + CHUNK)].bitcast(FP4X4),
-                        rhs_scale=picked_planes[a][:, chunk * CHUNK : (chunk + 1) * CHUNK],
+                        rhs_scale=planes[:, half, a, 0:PART].bitcast(U8)[:, j0 : j0 + CHUNK],
                         start=(a == 1),
                         stop=(a == 0),
                     )
@@ -290,26 +309,26 @@ def tile_list_gated_click_interests_kernel(tc, tab, offs, wv, wg_words, wg_scale
         gates = [(b, half, t) for b in range(2) for half in range(2) for t in range(4)]
         for b, half, t in gates[:8]:
             gate_tile(b, half, t)
-        round_wv(0, 0, nc.vector.tensor_copy, slice(0, 4))
+        round_wv(0, 0, nc.vector.tensor_copy, 0, 4)
         load_wo(0)
         permute_wg(1)
-        quantise_wv(0, 0)
-        round_wv(0, 1, nc.vector.tensor_copy, slice(0, 4))
+        quantise_wv(0, 0, 0, 4)
+        round_wv(0, 1, nc.vector.tensor_copy, 0, 4, AT_ROUNDED)
         load_wo(1)
-        quantise_wv(0, 1)
+        quantise_wv(0, 1, 0, 4)
         for b, half, t in gates[8:EARLY_GATES]:
             gate_tile(b, half, t)
-        round_wv(1, 0, nc.vector.tensor_copy, slice(0, 4))
-        round_wv(1, 1, nc.scalar.copy, slice(0, 4))
+        round_wv(1, 0, nc.vector.tensor_copy, 0, 4, AT_ROUNDED)
+        round_wv(1, 1, nc.scalar.copy, 0, 4)
         for b in range(2):
             round_wo(b)
 
         for chunk in range(CHUNKS):
             value_chunk(0, chunk)
             if chunk == 1:
-                quantise_wv(1, 0)
+                quantise_wv(1, 0, 0, 4)
             if chunk == 4:
-                quantise_wv(1, 1)
+                quantise_wv(1, 1, 0, 4)
             if chunk == 5:
                 quantise_h(0, 0, 4)
             if chunk == 7:

@@ -37,7 +37,7 @@ AT_TABLE = AT_PICKED1 + 2 * KIB
 AT_ROUNDED = AT_TABLE + 2 * RAW
 BANKS, BANK_BYTES = 8, 2048
 WARM_PASSES = (3, 3)
-EARLY_GATES = 12
+EARLY_GATES = 14
 BO_ROW = 32
 
 
@@ -190,9 +190,7 @@ def tile_list_gated_click_interests_kernel(tc, tab, offs, wv, wg_words, wg_scale
 
         def gate_tile(b, half, t):
             if t == 0:
-                name, shape = f"gate{b}{half}", [P, 4, HALF]
-                last = (b, half) == (1, 1)
-                gate[b, half] = placed(name, shape, F32, AT_WV0 + RAW) if last else sb(name, shape, F32)
+                gate[b, half] = sb(f"gate{b}{half}", [P, 4, HALF], F32)
             z = bank_tile((8 * b + 4 * half + t) % BANKS, [P, HALF])
             for a in range(2):
                 nc.tensor.matmul_mx(
@@ -233,7 +231,7 @@ def tile_list_gated_click_interests_kernel(tc, tab, offs, wv, wg_words, wg_scale
 
         def value_chunk(b, chunk):
             half, j0 = divmod(chunk * CHUNK, HALF)
-            val = bank_tile((chunk + 4) % BANKS if b == 0 else chunk % 4, [P, 4, CHUNK])
+            val = bank_tile((chunk + EARLY_GATES) % BANKS if b == 0 else chunk % 4, [P, 4, CHUNK])
             for t in range(4):
                 for a in (1, 0):
                     nc.tensor.matmul_mx(
@@ -266,17 +264,21 @@ def tile_list_gated_click_interests_kernel(tc, tab, offs, wv, wg_words, wg_scale
             for t in range(4):
                 nc.sync.dma_start(wo_raw[b][:, t, :], rows[t])
 
-        def round_wo(b):
-            wo_bf[b] = sb(f"wo_bf{b}", [P, 4 * N], BF16)
+        def round_wo(b, first, columns):
+            wo_bf[b, first] = sb(f"wo_bf{b}{first}", [P, 4 * columns], BF16)
             nc.scalar.copy(
-                wo_bf[b][:].rearrange("p (c u t) -> p c t u", u=4, t=4),
-                wo_raw[b][:].rearrange("p t (c u) -> p c t u", u=4),
+                wo_bf[b, first][:].rearrange("p (c u t) -> p c t u", u=4, t=4),
+                wo_raw[b][:, :, first : first + columns].rearrange("p t (c u) -> p c t u", u=4),
             )
 
-        def quantise_wo(b):
-            wo_codes[b] = sb(f"wo_codes{b}", [P, N], U32)
-            wo_planes[b] = sb(f"wo_planes{b}", [P, N], U8)
-            nc.vector.quantize_mx(out=wo_codes[b][:].bitcast(FP8X4), scales=wo_planes[b][:], in_=wo_bf[b][:])
+        def quantise_wo(b, first, columns):
+            if first == 0:
+                wo_codes[b] = sb(f"wo_codes{b}", [P, N], U32)
+                wo_planes[b] = sb(f"wo_planes{b}", [P, N], U8)
+            cols = slice(first, first + columns)
+            nc.vector.quantize_mx(
+                out=wo_codes[b][:, cols].bitcast(FP8X4), scales=wo_planes[b][:, cols], in_=wo_bf[b, first][:]
+            )
 
         out_rows = out.rearrange("(nt p) j -> p nt j", p=P)
 
@@ -320,8 +322,9 @@ def tile_list_gated_click_interests_kernel(tc, tab, offs, wv, wg_words, wg_scale
             gate_tile(b, half, t)
         round_wv(1, 0, nc.vector.tensor_copy, 0, 4, AT_ROUNDED)
         round_wv(1, 1, nc.scalar.copy, 0, 4)
-        for b in range(2):
-            round_wo(b)
+        round_wo(0, 0, N)
+        round_wo(1, 0, N // 2)
+        round_wo(1, N // 2, N // 2)
 
         for chunk in range(CHUNKS):
             value_chunk(0, chunk)
@@ -332,15 +335,16 @@ def tile_list_gated_click_interests_kernel(tc, tab, offs, wv, wg_words, wg_scale
             if chunk == 5:
                 quantise_h(0, 0, 4)
             if chunk == 7:
-                quantise_wo(0)
+                quantise_wo(0, 0, N)
         for b, half, t in gates[EARLY_GATES:]:
             gate_tile(b, half, t)
 
         value_chunk(1, 0)
         value_chunk(1, 1)
-        quantise_wo(1)
+        quantise_wo(1, 0, N // 2)
         quantise_h(1, 0, 2)
         value_chunk(1, 2)
+        quantise_wo(1, N // 2, N // 2)
         value_chunk(1, 3)
         out_piece(0)
         quantise_h(0, 4, 2)

@@ -28,16 +28,17 @@ RAW = 4 * PASS * 4
 PART = HALF // 4
 KIB = 1024
 AT_WG1 = 0
-AT_PICKED_SCALES = 3 * KIB // 2
 AT_WV0 = 2 * KIB
+AT_PICKED_SCALES = (AT_WV0, AT_WG1)
 AT_SCALE_ROWS = AT_WV0 + 2 * RAW - KIB
-AT_WG0 = AT_SCALE_ROWS + 2 * KIB
+AT_WV10 = AT_WV0 + 2 * RAW
+AT_WG0 = AT_WV10 + RAW - KIB
 AT_PICKED1 = AT_WG0 + KIB
-AT_TABLE = AT_PICKED1 + 2 * KIB
+AT_TABLE = AT_PICKED1 + 5 * KIB
 AT_ROUNDED = AT_TABLE + 2 * RAW
 BANKS, BANK_BYTES = 8, 2048
 WARM_PASSES = (3, 3)
-EARLY_GATES = 14
+EARLY_GATES = 13
 BO_ROW = 32
 
 
@@ -117,17 +118,16 @@ def tile_list_gated_click_interests_kernel(tc, tab, offs, wv, wg_words, wg_scale
             placed("scale_rows0", [P, 2 * PART], I32, AT_SCALE_ROWS),
             sb("scale_rows1", [P, 2 * PART], I32),
         ]
-        for b in range(2):
+
+        def pick_scales(part):
+            picked = placed(f"picked_scales{part}", [P, HALF], U8, AT_PICKED_SCALES[part])
+            list_cols = slice(HALF // 16 * part, HALF // 16 * (part + 1))
+            nc.vector.tensor_copy(picked[:], tab_scales[:].bitcast(U8).indirect(offsets[:, list_cols]))
             nc.vector.tensor_copy(
-                scale_rows[b][0:SCALE_ROWS, PART:].rearrange("p (t ph) -> p t ph", t=4),
-                wg_scale_rows[:, PART * b : PART * (b + 1)].rearrange("p (ph t) -> p t ph", t=4),
+                scale_rows[part][0:SCALE_ROWS, PART:].rearrange("p (t ph) -> p t ph", t=4),
+                wg_scale_rows[:, PART * part : PART * (part + 1)].rearrange("p (ph t) -> p t ph", t=4),
             )
-        picked_scales = placed("picked_scales", [P, S], U8, AT_PICKED_SCALES)
-        nc.vector.tensor_copy(picked_scales[:], tab_scales[:].bitcast(U8).indirect(offsets[:]))
-        for half in range(2):
-            nc.vector.tensor_copy(
-                scale_rows[half][:, 0:PART], picked_scales[:].bitcast(I32)[:, PART * half : PART * (half + 1)]
-            )
+            nc.vector.tensor_copy(scale_rows[part][:, 0:PART], picked[:].bitcast(I32))
 
         def move_planes(part):
             for q in range(4):
@@ -137,7 +137,7 @@ def tile_list_gated_click_interests_kernel(tc, tab, offs, wv, wg_words, wg_scale
 
         def load_wv(b, a):
             rows, cols = slice(PASS * a, PASS * (a + 1)), slice(PASS * b, PASS * (b + 1))
-            wv_raw[b, a] = placed(f"wv_raw{b}{a}", [P, 4, PASS], F32, (AT_WV0, AT_TABLE)[b] + a * RAW)
+            wv_raw[b, a] = placed(f"wv_raw{b}{a}", [P, 4, PASS], F32, AT_TABLE if (b, a) == (1, 1) else AT_WV0 + (2 * b + a) * RAW)
             nc.sync.dma_start(wv_raw[b, a][:], wv[rows, cols].rearrange("(p i) c -> p i c", i=4))
 
         def gather_words(half):
@@ -159,13 +159,16 @@ def tile_list_gated_click_interests_kernel(tc, tab, offs, wv, wg_words, wg_scale
             )
             wg_codes.append(codes)
 
+        pick_scales(0)
         move_planes(0)
         load_wv(0, 0)
+        pick_scales(1)
         move_planes(1)
         load_wg(1)
         load_wv(0, 1)
         gather_words(0)
         permute_wg(0)
+        load_wv(1, 0)
         part_words(0, slice(0, 1))
         part_words(0, slice(1, 2))
 
@@ -183,7 +186,6 @@ def tile_list_gated_click_interests_kernel(tc, tab, offs, wv, wg_words, wg_scale
 
         gather_words(1)
         part_words(1, slice(0, 2))
-        load_wv(1, 0)
         load_wv(1, 1)
 
         gate = {}
@@ -311,7 +313,7 @@ def tile_list_gated_click_interests_kernel(tc, tab, offs, wv, wg_words, wg_scale
         gates = [(b, half, t) for b in range(2) for half in range(2) for t in range(4)]
         for b, half, t in gates[:8]:
             gate_tile(b, half, t)
-        round_wv(0, 0, nc.vector.tensor_copy, 0, 4)
+        round_wv(0, 0, nc.vector.tensor_copy, 0, 4, AT_PICKED1 + KIB)
         load_wo(0)
         permute_wg(1)
         quantise_wv(0, 0, 0, 4)

@@ -22,7 +22,7 @@ PASS = 512
 HALF = 512
 CHUNK = 128
 CHUNKS = S // CHUNK
-PIECES = [(0, 256), (256, 256), (512, 256), (768, 128), (896, 128)]
+QUARTER = 256
 SCALE_ROWS = 32
 RAW = 4 * PASS * 4
 PART = HALF // 4
@@ -284,31 +284,48 @@ def tile_list_gated_click_interests_kernel(tc, tab, offs, wv, wg_words, wg_scale
 
         out_rows = out.rearrange("(nt p) j -> p nt j", p=P)
 
-        def out_piece(index):
-            j0, width = PIECES[index]
-            for nt0 in (0, 2):
-                acc = bank_tile(4 + (2 * index + nt0 // 2) % 4, [P, 2, width])
-                res = sb(f"res{index}{nt0}", [P, 2, width], F32)
-                for slot in range(2):
-                    cols = slice(P * (nt0 + slot), P * (nt0 + slot + 1))
-                    for b in (1, 0):
-                        nc.tensor.matmul_mx(
-                            out=acc[:, slot, :],
-                            lhsT=wo_codes[b][:, cols].bitcast(FP8X4),
-                            lhsT_scale=wo_planes[b][:, cols],
-                            rhs=h_codes[b][:, j0 : j0 + width].bitcast(FP8X4),
-                            rhs_scale=h_planes[b][:, j0 : j0 + width],
-                            start=(b == 1),
-                            stop=(b == 0),
-                        )
-                on_vector = index == len(PIECES) - 1 and nt0 == 0
-                for slot in range(2):
-                    bias = bias_cols[:, nt0 + slot, BO_ROW : BO_ROW + 1]
-                    if on_vector:
-                        nc.vector.tensor_scalar(res[:, slot, :], acc[:, slot, :], bias, None, ALU.add)
-                    else:
-                        nc.scalar.activation(res[:, slot, :], acc[:, slot, :], ACT.Identity, bias=bias)
-                nc.sync.dma_start(out_rows[:, nt0 : nt0 + 2, j0 : j0 + width], res[:])
+        def out_pass(acc, nt, b, j0, width, start, stop):
+            cols = slice(P * nt, P * (nt + 1))
+            nc.tensor.matmul_mx(
+                out=acc,
+                lhsT=wo_codes[b][:, cols].bitcast(FP8X4),
+                lhsT_scale=wo_planes[b][:, cols],
+                rhs=h_codes[b][:, j0 : j0 + width].bitcast(FP8X4),
+                rhs_scale=h_planes[b][:, j0 : j0 + width],
+                start=start,
+                stop=stop,
+            )
+
+        def add_bo(res, acc, nt, on_vector=False):
+            bias = bias_cols[:, nt, BO_ROW : BO_ROW + 1]
+            if on_vector:
+                nc.vector.tensor_scalar(res, acc, bias, None, ALU.add)
+            else:
+                nc.scalar.activation(res, acc, ACT.Identity, bias=bias)
+
+        def out_bank(j0, width, nt0, bank):
+            slots = HALF // width
+            acc = bank_tile(bank, [P, slots, width])
+            res = sb(f"res{j0}_{nt0}", [P, slots, width], F32)
+            for slot in range(slots):
+                for b in (1, 0):
+                    out_pass(acc[:, slot, :], nt0 + slot, b, j0, width, b == 1, b == 0)
+            for slot in range(slots):
+                add_bo(res[:, slot, :], acc[:, slot, :], nt0 + slot)
+            nc.sync.dma_start(out_rows[:, nt0 : nt0 + slots, j0 : j0 + width], res[:])
+
+        def last_piece(banks):
+            j0 = S - QUARTER
+            accs = [bank_tile(bank, [P, QUARTER]) for bank in banks]
+            for nt in range(4):
+                out_pass(accs[nt][:], nt, 0, j0, QUARTER, True, False)
+            for c0 in (0, CHUNK):
+                for nt in range(4):
+                    out_pass(accs[nt][:, c0 : c0 + CHUNK], nt, 1, j0 + c0, CHUNK, False, c0 == CHUNK)
+            for nt in range(4):
+                res = sb(f"res{j0}_{nt}", [P, QUARTER], F32)
+                add_bo(res[:], accs[nt][:], nt, on_vector=nt % 2 == 1)
+                nc.sync.dma_start(out_rows[:, nt, j0:S], res[:])
 
         gates = [(b, half, t) for b in range(2) for half in range(2) for t in range(4)]
         for b, half, t in gates[:8]:
@@ -348,18 +365,20 @@ def tile_list_gated_click_interests_kernel(tc, tab, offs, wv, wg_words, wg_scale
         value_chunk(1, 2)
         quantise_wo(1, N // 2, N // 2)
         value_chunk(1, 3)
-        out_piece(0)
+        out_bank(0, QUARTER, 0, 4)
+        out_bank(0, QUARTER, 2, 5)
         quantise_h(0, 4, 2)
         quantise_h(1, 2, 2)
         value_chunk(1, 4)
         value_chunk(1, 5)
-        out_piece(1)
+        out_bank(QUARTER, QUARTER, 0, 6)
+        out_bank(QUARTER, QUARTER, 2, 7)
         quantise_h(0, 6, 2)
         quantise_h(1, 4, 2)
         value_chunk(1, 6)
         value_chunk(1, 7)
-        out_piece(2)
+        out_bank(HALF, QUARTER, 0, 4)
+        out_bank(HALF, QUARTER, 2, 5)
         quantise_h(1, 6, 1)
-        out_piece(3)
         quantise_h(1, 7, 1)
-        out_piece(4)
+        last_piece((6, 7, 0, 1))

@@ -36,6 +36,7 @@ AT_WG0 = AT_WV10 + RAW - KIB
 AT_PICKED1 = AT_WG0 + KIB
 AT_TABLE = AT_PICKED1 + 5 * KIB
 AT_ROUNDED = AT_TABLE + 2 * RAW
+AT_PICKED0 = AT_ROUNDED + 5 * KIB
 BANKS, BANK_BYTES = 8, 2048
 WARM_PASSES = (3, 3)
 EARLY_GATES = 13
@@ -142,7 +143,7 @@ def tile_list_gated_click_interests_kernel(tc, tab, offs, wv, wg_words, wg_scale
 
         def gather_words(half):
             name, shape = f"picked{half}", [P, HALF]
-            picked = sb(name, shape, U32) if half == 0 else placed(name, shape, U32, AT_PICKED1)
+            picked = placed(name, shape, U32, (AT_PICKED0, AT_PICKED1)[half])
             list_cols = slice(HALF // 16 * half, HALF // 16 * (half + 1))
             nc.vector.tensor_copy(picked[:], tab_words[:].bitcast(U32).indirect(offsets[:, list_cols]))
             picked_words.append(picked[:].bitcast(U16).rearrange("p (j a) -> p a j", a=2))
@@ -185,7 +186,6 @@ def tile_list_gated_click_interests_kernel(tc, tab, offs, wv, wg_words, wg_scale
             )
 
         gather_words(1)
-        part_words(1, slice(0, 2))
         load_wv(1, 1)
 
         gate = {}
@@ -328,18 +328,23 @@ def tile_list_gated_click_interests_kernel(tc, tab, offs, wv, wg_words, wg_scale
                 nc.sync.dma_start(out_rows[:, nt, j0:S], res[:])
 
         gates = [(b, half, t) for b in range(2) for half in range(2) for t in range(4)]
+        round_wv(0, 0, nc.vector.tensor_copy, 0, 2, AT_PICKED0 - KIB)
+        part_words(1, slice(0, 2))
         for b, half, t in gates[:8]:
             gate_tile(b, half, t)
-        round_wv(0, 0, nc.vector.tensor_copy, 0, 4, AT_PICKED1 + KIB)
+        round_wv(0, 0, nc.vector.tensor_copy, 2, 2, AT_PICKED0 + KIB)
         load_wo(0)
+        quantise_wv(0, 0, 0, 2)
         permute_wg(1)
-        quantise_wv(0, 0, 0, 4)
-        round_wv(0, 1, nc.vector.tensor_copy, 0, 4, AT_ROUNDED)
+        quantise_wv(0, 0, 2, 2)
+        round_wv(0, 1, nc.vector.tensor_copy, 0, 2, AT_ROUNDED)
+        round_wv(0, 1, nc.vector.tensor_copy, 2, 2, AT_ROUNDED + 2 * KIB)
         load_wo(1)
-        quantise_wv(0, 1, 0, 4)
+        quantise_wv(0, 1, 0, 2)
+        quantise_wv(0, 1, 2, 2)
         for b, half, t in gates[8:EARLY_GATES]:
             gate_tile(b, half, t)
-        round_wv(1, 0, nc.vector.tensor_copy, 0, 4, AT_ROUNDED)
+        round_wv(1, 0, nc.vector.tensor_copy, 0, 4, AT_ROUNDED - 2 * KIB)
         round_wv(1, 1, nc.scalar.copy, 0, 4)
         round_wo(0, 0, N)
         round_wo(1, 0, N // 2)

@@ -246,9 +246,9 @@ def tile_list_gated_click_interests_kernel(tc, tab, offs, wv, wg_words, wg_scale
                         stop=(a == 0),
                     )
             nc.vector.tensor_tensor(
-                h_bf[b][:, 4 * CHUNK * chunk : 4 * CHUNK * (chunk + 1)].rearrange("p (c u t) -> p c t u", u=4, t=4),
-                val[:].rearrange("p t (c u) -> p c t u", u=4),
-                gate[b, half][:, :, j0 : j0 + CHUNK].rearrange("p t (c u) -> p c t u", u=4),
+                h_bf[b][:, 4 * CHUNK * chunk : 4 * CHUNK * (chunk + 1)].rearrange("p (c u t) -> p c t u", u=2, t=4),
+                val[:].rearrange("p t (c u) -> p c t u", u=2),
+                gate[b, half][:, :, j0 : j0 + CHUNK].rearrange("p t (c u) -> p c t u", u=2),
                 ALU.mult,
             )
 

@@ -38,9 +38,8 @@ AT_TABLE = AT_PICKED1 + 5 * KIB
 AT_ROUNDED = AT_TABLE + 2 * RAW
 AT_PICKED0 = AT_ROUNDED + 5 * KIB
 BANKS, BANK_BYTES = 8, 2048
-WARM_PASSES = (3, 3)
+WARM_PASSES = 2
 EARLY_GATES = 13
-BO_ROW = 32
 
 
 def tile_list_gated_click_interests_kernel(tc, tab, offs, wv, wg_words, wg_scales, bg, wo, bo, out):
@@ -88,16 +87,15 @@ def tile_list_gated_click_interests_kernel(tc, tab, offs, wv, wg_words, wg_scale
 
         warm_zero = sb("warm_zero", [P, 1], F32)
         nc.gpsimd.memset(warm_zero[:], 0.0)
+        bias_rows = sb("bias_rows", [P, 4, P], F32)
+        nc.gpsimd.memset(bias_rows[:], 0.0)
         nc.vector.memset(tab_scales[32:64, :], 0)
         nc.gpsimd.memset(tab_scales[64:P, :], 0)
         planes = sb("planes", [P, 2, 2, 2 * PART], I32)
         nc.vector.memset(planes[:], 0)
 
-        bias_in = sb("bias_in", [BO_ROW + 1, PASS], F32)
-        nc.scalar.dma_start(bias_in[0:2], bg.rearrange("(b c) -> b c", b=2))
-        nc.scalar.dma_start(bias_in[BO_ROW : BO_ROW + 1], bo.rearrange("(o n) -> o n", o=1))
-        bias_rows = sb("bias_rows", [P, 4, P], F32)
-        nc.gpsimd.memset(bias_rows[:], 0.0)
+        bias_in = sb("bias_in", [2, PASS], F32)
+        nc.scalar.dma_start(bias_in[:], bg.rearrange("(b c) -> b c", b=2))
         identity = sb("identity", [P, P], F32)
         make_identity(nc, identity[:])
 
@@ -106,14 +104,13 @@ def tile_list_gated_click_interests_kernel(tc, tab, offs, wv, wg_words, wg_scale
 
         nc.scalar.copy(
             bias_rows[0:2].rearrange("b t (ph el) -> b t ph el", el=4),
-            bias_in[0:2].rearrange("b (ph t el) -> b t ph el", t=4, el=4),
+            bias_in[:].rearrange("b (ph t el) -> b t ph el", t=4, el=4),
         )
-        nc.scalar.copy(bias_rows[BO_ROW : BO_ROW + 1].rearrange("o c p -> o (c p)"), bias_in[BO_ROW : BO_ROW + 1])
         turned = last_bank("turned", [P, 4, P])
         for t in range(4):
             nc.tensor.transpose(turned[:, t, :], bias_rows[:, t, :], identity[:])
-        bias_cols = sb("bias_cols", [P, 4, BO_ROW + 1], F32)
-        nc.scalar.copy(bias_cols[:], turned[:, :, 0 : BO_ROW + 1])
+        bias_cols = sb("bias_cols", [P, 4, 2], F32)
+        nc.scalar.copy(bias_cols[:], turned[:, :, 0:2])
 
         scale_rows = [
             placed("scale_rows0", [P, 2 * PART], I32, AT_SCALE_ROWS),
@@ -153,10 +150,11 @@ def tile_list_gated_click_interests_kernel(tc, tab, offs, wv, wg_words, wg_scale
             nc.vector.tensor_copy(picked_codes[half][:].bitcast(U16)[:, passes], picked_words[half][:, passes])
 
         def permute_wg(b):
-            codes = sb(f"wg_codes{b}", [P, 2, 4, P // 2], I32)
-            nc.vector.tensor_copy(
-                codes[:].rearrange("p a t (ph e) -> p a t ph e", e=2),
-                wg_raw[b][:].rearrange("p a (ph t e) -> p a t ph e", t=4, e=2),
+            codes = sb(f"wg_codes{b}", [P, 2, 4, P // 2], I32, tag="bias_rows" if b == 0 else None)
+            copy = nc.scalar.copy if b == 0 else nc.vector.tensor_copy
+            copy(
+                codes[:].bitcast(U32).rearrange("p a t (ph e) -> p a t ph e", e=2),
+                wg_raw[b][:].bitcast(U32).rearrange("p a (ph t e) -> p a t ph e", t=4, e=2),
             )
             wg_codes.append(codes)
 
@@ -174,7 +172,7 @@ def tile_list_gated_click_interests_kernel(tc, tab, offs, wv, wg_words, wg_scale
         part_words(0, slice(1, 2))
 
         warm_bank = last_bank("warm_bank", [P, HALF])
-        for words in [scale_rows[1]] * WARM_PASSES[0] + [tab_words] * WARM_PASSES[1]:
+        for words in [scale_rows[0]] * WARM_PASSES + [scale_rows[1]] * WARM_PASSES + [tab_words] * WARM_PASSES:
             nc.tensor.matmul_mx(
                 out=warm_bank[:],
                 lhsT=words[:, 0 : P // 2].bitcast(FP4X4),
@@ -297,7 +295,7 @@ def tile_list_gated_click_interests_kernel(tc, tab, offs, wv, wg_words, wg_scale
             )
 
         def add_bo(res, acc, nt, on_vector=False):
-            bias = bias_cols[:, nt, BO_ROW : BO_ROW + 1]
+            bias = bo_cols[:, nt : nt + 1]
             if on_vector:
                 nc.vector.tensor_scalar(res, acc, bias, None, ALU.add)
             else:
@@ -346,6 +344,9 @@ def tile_list_gated_click_interests_kernel(tc, tab, offs, wv, wg_words, wg_scale
             gate_tile(b, half, t)
         round_wv(1, 0, nc.vector.tensor_copy, 0, 4, AT_ROUNDED - 2 * KIB)
         round_wv(1, 1, nc.scalar.copy, 0, 4)
+        bo_cols = placed("bo_cols", [P, 4], F32, AT_TABLE)
+        with nc.allow_non_contiguous_dma(reason="one value a partition"):
+            nc.sync.dma_start(bo_cols[:], bo.rearrange("(nt p) -> p nt", p=P))
         round_wo(0, 0, N)
         round_wo(1, 0, N // 2)
         round_wo(1, N // 2, N // 2)

@@ -32,9 +32,10 @@ AT_WV0 = 2 * KIB
 AT_PICKED_SCALES = (AT_WV0, AT_WG1)
 AT_SCALE_ROWS = AT_WV0 + 2 * RAW - KIB
 AT_WV10 = AT_WV0 + 2 * RAW
-AT_WG0 = AT_WV10 + RAW - KIB
-AT_PICKED1 = AT_WG0 + KIB
-AT_TABLE = AT_PICKED1 + 5 * KIB
+AT_WG0 = AT_WV10 + RAW - 64
+AT_PICKED1 = AT_WG0 + 2 * KIB - 64
+AT_WV00_ROUNDED = AT_WG0 + 64
+AT_TABLE = AT_WV00_ROUNDED + 4 * KIB
 AT_ROUNDED = AT_TABLE + 2 * RAW
 AT_PICKED0 = AT_ROUNDED + 5 * KIB
 BANKS, BANK_BYTES = 8, 2048
@@ -216,7 +217,8 @@ def tile_list_gated_click_interests_kernel(tc, tab, offs, wv, wg_words, wg_scale
 
         def quantise_wv(b, a, first, slots):
             if first == 0:
-                wv_codes[b, a] = sb(f"wv_codes{b}{a}", [P, PASS], U32)
+                name, shape = f"wv_codes{b}{a}", [P, PASS]
+                wv_codes[b, a] = placed(name, shape, U32, AT_WG1) if b + a == 0 else sb(name, shape, U32)
                 wv_planes[b, a] = sb(f"wv_planes{b}{a}", [P, PASS], U8)
             cols = slice(P * first, P * (first + slots))
             nc.vector.quantize_mx(
@@ -326,14 +328,15 @@ def tile_list_gated_click_interests_kernel(tc, tab, offs, wv, wg_words, wg_scale
                 nc.sync.dma_start(out_rows[:, nt, j0:S], res[:])
 
         gates = [(b, half, t) for b in range(2) for half in range(2) for t in range(4)]
-        round_wv(0, 0, nc.vector.tensor_copy, 0, 2, AT_PICKED0 - KIB)
-        part_words(1, slice(0, 2))
+        part_words(1, slice(0, 1))
+        part_words(1, slice(1, 2))
+        round_wv(0, 0, nc.vector.tensor_copy, 0, 2, AT_WV00_ROUNDED)
         for b, half, t in gates[:8]:
             gate_tile(b, half, t)
-        round_wv(0, 0, nc.vector.tensor_copy, 2, 2, AT_PICKED0 + KIB)
+        round_wv(0, 0, nc.vector.tensor_copy, 2, 2, AT_WV00_ROUNDED + 2 * KIB)
         load_wo(0)
-        quantise_wv(0, 0, 0, 2)
         permute_wg(1)
+        quantise_wv(0, 0, 0, 2)
         quantise_wv(0, 0, 2, 2)
         round_wv(0, 1, nc.vector.tensor_copy, 0, 2, AT_ROUNDED)
         round_wv(0, 1, nc.vector.tensor_copy, 2, 2, AT_ROUNDED + 2 * KIB)
@@ -342,7 +345,8 @@ def tile_list_gated_click_interests_kernel(tc, tab, offs, wv, wg_words, wg_scale
         quantise_wv(0, 1, 2, 2)
         for b, half, t in gates[8:EARLY_GATES]:
             gate_tile(b, half, t)
-        round_wv(1, 0, nc.vector.tensor_copy, 0, 4, AT_ROUNDED - 2 * KIB)
+        round_wv(1, 0, nc.vector.tensor_copy, 0, 2, AT_ROUNDED)
+        round_wv(1, 0, nc.scalar.copy, 2, 2)
         round_wv(1, 1, nc.scalar.copy, 0, 4)
         bo_cols = placed("bo_cols", [P, 4], F32, AT_TABLE)
         with nc.allow_non_contiguous_dma(reason="one value a partition"):
@@ -353,12 +357,14 @@ def tile_list_gated_click_interests_kernel(tc, tab, offs, wv, wg_words, wg_scale
 
         for chunk in range(CHUNKS):
             value_chunk(0, chunk)
-            if chunk == 1:
-                quantise_wv(1, 0, 0, 4)
+            if chunk == 0:
+                quantise_wv(1, 0, 0, 2)
+            if chunk == 2:
+                quantise_wv(1, 0, 2, 2)
             if chunk == 4:
-                quantise_wv(1, 1, 0, 4)
-            if chunk == 5:
                 quantise_h(0, 0, 4)
+            if chunk == 5:
+                quantise_wv(1, 1, 0, 4)
             if chunk == 7:
                 quantise_wo(0, 0, N)
         for b, half, t in gates[EARLY_GATES:]:

@@ -227,12 +227,23 @@ def tile_list_gated_click_interests_kernel(tc, tab, offs, wv, wg_words, wg_scale
                 in_=wv_bf[b, a, first][:].rearrange("p t c -> p (t c)"),
             )
 
-        h_bf = [sb(f"h_bf{b}", [P, 4 * S], BF16) for b in range(2)]
-        h_codes = [sb(f"h_codes{b}", [P, S], U32) for b in range(2)]
+        h_calls = ((0, 0, 4), (0, 4, 4), (1, 0, 4), (1, 4, 2), (1, 6, 1), (1, 7, 1))
+        h_bf, h_home = {}, {}
+        for b, first, chunks in h_calls:
+            tag = "h_bf14" if (b, first) == (1, 7) else None
+            h_bf[b, first] = sb(f"h_bf{b}{first}", [P, 4 * CHUNK * chunks], BF16, tag=tag)
+            for chunk in range(first, first + chunks):
+                h_home[b, chunk] = first
+        h_codes = {
+            (b, half): sb(f"h_codes{b}{half}", [P, HALF], U32, tag="h_bf10" if (b, half) == (0, 1) else None)
+            for b in range(2)
+            for half in range(2)
+        }
         h_planes = [sb(f"h_planes{b}", [P, S], U8) for b in range(2)]
 
         def value_chunk(b, chunk):
             half, j0 = divmod(chunk * CHUNK, HALF)
+            at = 4 * CHUNK * (chunk - h_home[b, chunk])
             val = bank_tile((chunk + EARLY_GATES) % BANKS if b == 0 else chunk % 4, [P, 4, CHUNK])
             for t in range(4):
                 for a in (1, 0):
@@ -246,7 +257,7 @@ def tile_list_gated_click_interests_kernel(tc, tab, offs, wv, wg_words, wg_scale
                         stop=(a == 0),
                     )
             nc.vector.tensor_tensor(
-                h_bf[b][:, 4 * CHUNK * chunk : 4 * CHUNK * (chunk + 1)].rearrange("p (c u t) -> p c t u", u=2, t=4),
+                h_bf[b, h_home[b, chunk]][:, at : at + 4 * CHUNK].rearrange("p (c u t) -> p c t u", u=2, t=4),
                 val[:].rearrange("p t (c u) -> p c t u", u=2),
                 gate[b, half][:, :, j0 : j0 + CHUNK].rearrange("p t (c u) -> p c t u", u=2),
                 ALU.mult,
@@ -255,7 +266,7 @@ def tile_list_gated_click_interests_kernel(tc, tab, offs, wv, wg_words, wg_scale
         def quantise_h(b, first_chunk, chunks):
             j0, j1 = first_chunk * CHUNK, (first_chunk + chunks) * CHUNK
             nc.vector.quantize_mx(
-                out=h_codes[b][:, j0:j1].bitcast(FP8X4), scales=h_planes[b][:, j0:j1], in_=h_bf[b][:, 4 * j0 : 4 * j1]
+                out=h_codes[b, j0 // HALF][:, j0 % HALF : j0 % HALF + j1 - j0].bitcast(FP8X4), scales=h_planes[b][:, j0:j1], in_=h_bf[b, first_chunk][:]
             )
 
         wo_raw, wo_bf, wo_codes, wo_planes = {}, {}, {}, {}
@@ -290,7 +301,7 @@ def tile_list_gated_click_interests_kernel(tc, tab, offs, wv, wg_words, wg_scale
                 out=acc,
                 lhsT=wo_codes[b][:, cols].bitcast(FP8X4),
                 lhsT_scale=wo_planes[b][:, cols],
-                rhs=h_codes[b][:, j0 : j0 + width].bitcast(FP8X4),
+                rhs=h_codes[b, j0 // HALF][:, j0 % HALF : j0 % HALF + width].bitcast(FP8X4),
                 rhs_scale=h_planes[b][:, j0 : j0 + width],
                 start=start,
                 stop=stop,
@@ -303,13 +314,12 @@ def tile_list_gated_click_interests_kernel(tc, tab, offs, wv, wg_words, wg_scale
             else:
                 nc.scalar.activation(res, acc, ACT.Identity, bias=bias)
 
-        def out_bank(j0, width, nt0, bank):
-            slots = HALF // width
+        def out_bank(j0, width, nt0, slots, bank):
             acc = bank_tile(bank, [P, slots, width])
             res = sb(f"res{j0}_{nt0}", [P, slots, width], F32)
-            for slot in range(slots):
-                for b in (1, 0):
-                    out_pass(acc[:, slot, :], nt0 + slot, b, j0, width, b == 1, b == 0)
+            for b in range(2):
+                for slot in range(slots):
+                    out_pass(acc[:, slot, :], nt0 + slot, b, j0, width, b + slot == 0, b + slot == slots)
             for slot in range(slots):
                 add_bo(res[:, slot, :], acc[:, slot, :], nt0 + slot)
             nc.sync.dma_start(out_rows[:, nt0 : nt0 + slots, j0 : j0 + width], res[:])
@@ -370,27 +380,21 @@ def tile_list_gated_click_interests_kernel(tc, tab, offs, wv, wg_words, wg_scale
         for b, half, t in gates[EARLY_GATES:]:
             gate_tile(b, half, t)
 
-        value_chunk(1, 0)
-        value_chunk(1, 1)
+        for chunk in range(4):
+            value_chunk(1, chunk)
         quantise_wo(1, 0, N // 2)
-        quantise_h(1, 0, 2)
-        value_chunk(1, 2)
+        quantise_h(1, 0, 4)
         quantise_wo(1, N // 2, N // 2)
-        value_chunk(1, 3)
-        out_bank(0, QUARTER, 0, 4)
-        out_bank(0, QUARTER, 2, 5)
-        quantise_h(0, 4, 2)
-        quantise_h(1, 2, 2)
         value_chunk(1, 4)
         value_chunk(1, 5)
-        out_bank(QUARTER, QUARTER, 0, 6)
-        out_bank(QUARTER, QUARTER, 2, 7)
-        quantise_h(0, 6, 2)
-        quantise_h(1, 4, 2)
+        for nt in range(4):
+            out_bank(0, HALF, nt, 1, 4 + nt)
+        quantise_h(0, 4, 4)
         value_chunk(1, 6)
+        quantise_h(1, 4, 2)
         value_chunk(1, 7)
-        out_bank(HALF, QUARTER, 0, 4)
-        out_bank(HALF, QUARTER, 2, 5)
+        out_bank(HALF, QUARTER, 0, 2, 4)
+        out_bank(HALF, QUARTER, 2, 2, 5)
         quantise_h(1, 6, 1)
         quantise_h(1, 7, 1)
-        last_piece((6, 7, 0, 1))
+        last_piece((0, 1, 6, 2))

from contextlib import ExitStack

import concourse.mybir as mybir
from concourse.masks import make_identity

K, T, S, H, N = 1024, 4096, 1024, 1024, 512
FLOPS = 2 * (2 * K * H * S + H * N * S)

F32 = mybir.dt.float32
BF16 = mybir.dt.bfloat16
I32 = mybir.dt.int32
U32 = mybir.dt.uint32
U16 = mybir.dt.uint16
U8 = mybir.dt.uint8
FP8X4 = mybir.dt.float8_e4m3fn_x4
FP4X4 = mybir.dt.float4_e2m1fn_x4
ACT = mybir.ActivationFunctionType
ALU = mybir.AluOpType

P = 128
PASS = 512
HALF = 512
CHUNK = 128
CHUNKS = S // CHUNK
QUARTER = 256
SCALE_ROWS = 32
RAW = 4 * PASS * 4
PART = HALF // 4
KIB = 1024
AT_WG1 = 0
AT_WV0 = 2 * KIB
AT_PICKED_SCALES = (AT_WV0, AT_WG1)
AT_SCALE_ROWS = AT_WV0 + 2 * RAW - KIB
AT_WV10 = AT_WV0 + 2 * RAW
AT_WG0 = AT_WV10 + RAW - 64
AT_PICKED1 = AT_WG0 + 2 * KIB - 64
AT_WV00_ROUNDED = AT_WG0 + 64
AT_TABLE = AT_WV00_ROUNDED + 4 * KIB
AT_ROUNDED = AT_TABLE + 2 * RAW
AT_PICKED0 = AT_ROUNDED + 5 * KIB
BANKS, BANK_BYTES = 8, 2048
WARM_PASSES = 2
EARLY_GATES = 13


def tile_list_gated_click_interests_kernel(tc, tab, offs, wv, wg_words, wg_scales, bg, wo, bo, out):
    nc = tc.nc
    with ExitStack() as ctx:
        keep = ctx.enter_context(tc.tile_pool(name="keep", bufs=1))
        turns = ctx.enter_context(tc.tile_pool(name="turns", bufs=1))
        psum = ctx.enter_context(tc.psum_pool(name="psum", bufs=1))

        banks_taken = []

        def bank_tile(bank, shape):
            banks_taken.append(bank)
            return psum.tile(shape, F32, name=f"sums{len(banks_taken)}", offset=BANK_BYTES * bank)

        def last_bank(name, shape):
            return psum.tile(shape, F32, name=name, offset=BANK_BYTES * (BANKS - 1))

        def sb(name, shape, dt, tag=None):
            return keep.tile(shape, dt, name=name, tag=tag or name, align_bytes=64)

        def placed(name, shape, dt, offset):
            return turns.tile(shape, dt, name=name, align_bytes=64, offset=offset)

        offsets = keep.tile([P, S // 16], U16, name="offsets")
        nc.sync.dma_start(offsets[:], offs)

        tab32 = tab.bitcast(I32)
        tab_scales = sb("tab_scales", [P, T // 4], I32)
        nc.sync.dma_start(
            tab_scales[0:SCALE_ROWS, :], tab32[0, P * T :].rearrange("(a r t) -> r a t", a=2, r=16)
        )
        wg_scale_rows = sb("wg_scale_rows", [SCALE_ROWS, H // 4], I32)
        nc.sync.dma_start(wg_scale_rows[:], wg_scales.bitcast(I32).rearrange("a r w -> r a w"))
        tab_words = placed("tab_words", [P, T], I32, AT_TABLE)
        nc.sync.dma_start(tab_words[:], tab32[0, 0 : P * T].rearrange("(p t) -> p t", p=P))
        wg32 = wg_words.bitcast(I32).rearrange("a p w -> p a w")
        wg_raw = []

        def load_wg(b):
            wg_raw.append(placed(f"wg_raw{b}", [P, 2, 256], I32, (AT_WG0, AT_WG1)[b]))
            nc.sync.dma_start(wg_raw[b][:], wg32[:, :, 256 * b : 256 * (b + 1)])

        load_wg(0)

        warm_zero = sb("warm_zero", [P, 1], F32)
        nc.gpsimd.memset(warm_zero[:], 0.0)
        bias_rows = sb("bias_rows", [P, 4, P], F32)
        nc.gpsimd.memset(bias_rows[:], 0.0)
        nc.vector.memset(tab_scales[32:64, :], 0)
        nc.gpsimd.memset(tab_scales[64:P, :], 0)
        planes = sb("planes", [P, 2, 2, 2 * PART], I32)
        nc.vector.memset(planes[:], 0)

        bias_in = sb("bias_in", [2, PASS], F32)
        nc.scalar.dma_start(bias_in[:], bg.rearrange("(b c) -> b c", b=2))
        identity = sb("identity", [P, P], F32)
        make_identity(nc, identity[:])

        warm_column = sb("warm_column", [P, 1], F32)
        nc.scalar.activation(warm_column[:], warm_zero[:], ACT.Sigmoid)

        nc.scalar.copy(
            bias_rows[0:2].rearrange("b t (ph el) -> b t ph el", el=4),
            bias_in[:].rearrange("b (ph t el) -> b t ph el", t=4, el=4),
        )
        turned = last_bank("turned", [P, 4, P])
        for t in range(4):
            nc.tensor.transpose(turned[:, t, :], bias_rows[:, t, :], identity[:])
        bias_cols = sb("bias_cols", [P, 4, 2], F32)
        nc.scalar.copy(bias_cols[:], turned[:, :, 0:2])

        scale_rows = [
            placed("scale_rows0", [P, 2 * PART], I32, AT_SCALE_ROWS),
            sb("scale_rows1", [P, 2 * PART], I32),
        ]

        def pick_scales(part):
            picked = placed(f"picked_scales{part}", [P, HALF], U8, AT_PICKED_SCALES[part])
            list_cols = slice(HALF // 16 * part, HALF // 16 * (part + 1))
            nc.vector.tensor_copy(picked[:], tab_scales[:].bitcast(U8).indirect(offsets[:, list_cols]))
            nc.vector.tensor_copy(
                scale_rows[part][0:SCALE_ROWS, PART:].rearrange("p (t ph) -> p t ph", t=4),
                wg_scale_rows[:, PART * part : PART * (part + 1)].rearrange("p (ph t) -> p t ph", t=4),
            )
            nc.vector.tensor_copy(scale_rows[part][:, 0:PART], picked[:].bitcast(I32))

        def move_planes(part):
            for q in range(4):
                nc.sync.dma_start(planes[32 * q : 32 * q + 4, part], scale_rows[part][8 * q : 8 * q + 8, :])

        wv_raw, picked_words, picked_codes, wg_codes = {}, [], [], []

        def load_wv(b, a):
            rows, cols = slice(PASS * a, PASS * (a + 1)), slice(PASS * b, PASS * (b + 1))
            wv_raw[b, a] = placed(f"wv_raw{b}{a}", [P, 4, PASS], F32, AT_TABLE if (b, a) == (1, 1) else AT_WV0 + (2 * b + a) * RAW)
            nc.sync.dma_start(wv_raw[b, a][:], wv[rows, cols].rearrange("(p i) c -> p i c", i=4))

        def gather_words(half):
            name, shape = f"picked{half}", [P, HALF]
            picked = placed(name, shape, U32, (AT_PICKED0, AT_PICKED1)[half])
            list_cols = slice(HALF // 16 * half, HALF // 16 * (half + 1))
            nc.vector.tensor_copy(picked[:], tab_words[:].bitcast(U32).indirect(offsets[:, list_cols]))
            picked_words.append(picked[:].bitcast(U16).rearrange("p (j a) -> p a j", a=2))
            picked_codes.append(sb(f"parted{half}", [P, 2, 2 * HALF], U8))

        def part_words(half, passes):
            nc.vector.tensor_copy(picked_codes[half][:].bitcast(U16)[:, passes], picked_words[half][:, passes])

        def permute_wg(b):
            codes = sb(f"wg_codes{b}", [P, 2, 4, P // 2], I32, tag="bias_rows" if b == 0 else None)
            copy = nc.scalar.copy if b == 0 else nc.vector.tensor_copy
            copy(
                codes[:].bitcast(U32).rearrange("p a t (ph e) -> p a t ph e", e=2),
                wg_raw[b][:].bitcast(U32).rearrange("p a (ph t e) -> p a t ph e", t=4, e=2),
            )
            wg_codes.append(codes)

        pick_scales(0)
        move_planes(0)
        load_wv(0, 0)
        pick_scales(1)
        move_planes(1)
        load_wg(1)
        load_wv(0, 1)
        gather_words(0)
        permute_wg(0)
        load_wv(1, 0)
        part_words(0, slice(0, 1))
        part_words(0, slice(1, 2))

        warm_bank = last_bank("warm_bank", [P, HALF])
        for words in [scale_rows[0]] * WARM_PASSES + [scale_rows[1]] * WARM_PASSES + [tab_words] * WARM_PASSES:
            nc.tensor.matmul_mx(
                out=warm_bank[:],
                lhsT=words[:, 0 : P // 2].bitcast(FP4X4),
                lhsT_scale=tab_scales[:, 0 : P // 4].bitcast(U8),
                rhs=tab_scales[:, 0 : HALF // 2].bitcast(FP4X4),
                rhs_scale=tab_scales[:, 0 : HALF // 4].bitcast(U8),
                start=True,
                stop=True,
            )

        gather_words(1)
        load_wv(1, 1)

        gate = {}

        def gate_tile(b, half, t):
            if t == 0:
                gate[b, half] = sb(f"gate{b}{half}", [P, 4, HALF], F32)
            z = bank_tile((8 * b + 4 * half + t) % BANKS, [P, HALF])
            for a in range(2):
                nc.tensor.matmul_mx(
                    out=z[:],
                    lhsT=wg_codes[b][:, a, t, :].bitcast(FP4X4),
                    lhsT_scale=planes[:, b, a, PART + 32 * t : PART + 32 * (t + 1)].bitcast(U8),
                    rhs=picked_codes[half][:, a, :].bitcast(FP4X4),
                    rhs_scale=planes[:, half, a, 0:PART].bitcast(U8),
                    start=(a == 0),
                    stop=(a == 1),
                )
            nc.scalar.activation(gate[b, half][:, t, :], z[:], ACT.Sigmoid, bias=bias_cols[:, t, b : b + 1])

        wv_bf, wv_codes, wv_planes = {}, {}, {}

        def round_wv(b, a, copy, first, slots, at=None):
            name, shape = f"wv_bf{b}{a}{first}", [P, slots, PASS]
            wv_bf[b, a, first] = sb(name, shape, BF16) if at is None else placed(name, shape, BF16, at)
            copy(
                wv_bf[b, a, first][:].rearrange("p t (ph el i) -> p t ph i el", el=4, i=4),
                wv_raw[b, a][:].rearrange("p i (ph t el) -> p t ph i el", t=4, el=4)[:, first : first + slots],
            )

        def quantise_wv(b, a, first, slots):
            if first == 0:
                name, shape = f"wv_codes{b}{a}", [P, PASS]
                wv_codes[b, a] = placed(name, shape, U32, AT_WG1) if b + a == 0 else sb(name, shape, U32)
                wv_planes[b, a] = sb(f"wv_planes{b}{a}", [P, PASS], U8)
            cols = slice(P * first, P * (first + slots))
            nc.vector.quantize_mx(
                out=wv_codes[b, a][:, cols].bitcast(FP8X4),
                scales=wv_planes[b, a][:, cols],
                in_=wv_bf[b, a, first][:].rearrange("p t c -> p (t c)"),
            )

        h_calls = ((0, 0, 4), (0, 4, 4), (1, 0, 4), (1, 4, 2), (1, 6, 1), (1, 7, 1))
        h_bf, h_home = {}, {}
        for b, first, chunks in h_calls:
            tag = "h_bf14" if (b, first) == (1, 7) else None
            h_bf[b, first] = sb(f"h_bf{b}{first}", [P, 4 * CHUNK * chunks], BF16, tag=tag)
            for chunk in range(first, first + chunks):
                h_home[b, chunk] = first
        h_codes = {
            (b, half): sb(f"h_codes{b}{half}", [P, HALF], U32, tag="h_bf10" if (b, half) == (0, 1) else None)
            for b in range(2)
            for half in range(2)
        }
        h_planes = [sb(f"h_planes{b}", [P, S], U8) for b in range(2)]

        def value_chunk(b, chunk):
            half, j0 = divmod(chunk * CHUNK, HALF)
            at = 4 * CHUNK * (chunk - h_home[b, chunk])
            val = bank_tile((chunk + EARLY_GATES) % BANKS if b == 0 else chunk % 4, [P, 4, CHUNK])
            for t in range(4):
                for a in (1, 0):
                    nc.tensor.matmul_mx(
                        out=val[:, t, :],
                        lhsT=wv_codes[b, a][:, P * t : P * (t + 1)].bitcast(FP8X4),
                        lhsT_scale=wv_planes[b, a][:, P * t : P * (t + 1)],
                        rhs=picked_codes[half][:, a, 2 * j0 : 2 * (j0 + CHUNK)].bitcast(FP4X4),
                        rhs_scale=planes[:, half, a, 0:PART].bitcast(U8)[:, j0 : j0 + CHUNK],
                        start=(a == 1),
                        stop=(a == 0),
                    )
            nc.vector.tensor_tensor(
                h_bf[b, h_home[b, chunk]][:, at : at + 4 * CHUNK].rearrange("p (c u t) -> p c t u", u=2, t=4),
                val[:].rearrange("p t (c u) -> p c t u", u=2),
                gate[b, half][:, :, j0 : j0 + CHUNK].rearrange("p t (c u) -> p c t u", u=2),
                ALU.mult,
            )

        def quantise_h(b, first_chunk, chunks):
            j0, j1 = first_chunk * CHUNK, (first_chunk + chunks) * CHUNK
            nc.vector.quantize_mx(
                out=h_codes[b, j0 // HALF][:, j0 % HALF : j0 % HALF + j1 - j0].bitcast(FP8X4), scales=h_planes[b][:, j0:j1], in_=h_bf[b, first_chunk][:]
            )

        wo_raw, wo_bf, wo_codes, wo_planes = {}, {}, {}, {}

        def load_wo(b):
            wo_raw[b] = placed(f"wo_raw{b}", [P, 4, N], F32, AT_WV0 + b * RAW)
            rows = wo[PASS * b : PASS * (b + 1), :].rearrange("(ph t el) n -> t ph el n", t=4, el=4)
            for t in range(4):
                nc.sync.dma_start(wo_raw[b][:, t, :], rows[t])

        def round_wo(b, first, columns):
            wo_bf[b, first] = sb(f"wo_bf{b}{first}", [P, 4 * columns], BF16)
            nc.scalar.copy(
                wo_bf[b, first][:].rearrange("p (c u t) -> p c t u", u=4, t=4),
                wo_raw[b][:, :, first : first + columns].rearrange("p t (c u) -> p c t u", u=4),
            )

        def quantise_wo(b, first, columns):
            if first == 0:
                wo_codes[b] = sb(f"wo_codes{b}", [P, N], U32)
                wo_planes[b] = sb(f"wo_planes{b}", [P, N], U8)
            cols = slice(first, first + columns)
            nc.vector.quantize_mx(
                out=wo_codes[b][:, cols].bitcast(FP8X4), scales=wo_planes[b][:, cols], in_=wo_bf[b, first][:]
            )

        out_rows = out.rearrange("(nt p) j -> p nt j", p=P)

        def out_pass(acc, nt, b, j0, width, start, stop):
            cols = slice(P * nt, P * (nt + 1))
            nc.tensor.matmul_mx(
                out=acc,
                lhsT=wo_codes[b][:, cols].bitcast(FP8X4),
                lhsT_scale=wo_planes[b][:, cols],
                rhs=h_codes[b, j0 // HALF][:, j0 % HALF : j0 % HALF + width].bitcast(FP8X4),
                rhs_scale=h_planes[b][:, j0 : j0 + width],
                start=start,
                stop=stop,
            )

        def add_bo(res, acc, nt, on_vector=False):
            bias = bo_cols[:, nt : nt + 1]
            if on_vector:
                nc.vector.tensor_scalar(res, acc, bias, None, ALU.add)
            else:
                nc.scalar.activation(res, acc, ACT.Identity, bias=bias)

        def out_bank(j0, width, nt0, slots, bank):
            acc = bank_tile(bank, [P, slots, width])
            res = sb(f"res{j0}_{nt0}", [P, slots, width], F32)
            for b in range(2):
                for slot in range(slots):
                    out_pass(acc[:, slot, :], nt0 + slot, b, j0, width, b + slot == 0, b + slot == slots)
            for slot in range(slots):
                add_bo(res[:, slot, :], acc[:, slot, :], nt0 + slot)
            nc.sync.dma_start(out_rows[:, nt0 : nt0 + slots, j0 : j0 + width], res[:])

        def last_piece(banks):
            j0 = S - QUARTER
            accs = [bank_tile(bank, [P, QUARTER]) for bank in banks]
            for nt in range(4):
                out_pass(accs[nt][:], nt, 0, j0, QUARTER, True, False)
            for c0 in (0, CHUNK):
                for nt in range(4):
                    out_pass(accs[nt][:, c0 : c0 + CHUNK], nt, 1, j0 + c0, CHUNK, False, c0 == CHUNK)
            for nt in range(4):
                res = sb(f"res{j0}_{nt}", [P, QUARTER], F32)
                add_bo(res[:], accs[nt][:], nt, on_vector=nt % 2 == 1)
                nc.sync.dma_start(out_rows[:, nt, j0:S], res[:])

        gates = [(b, half, t) for b in range(2) for half in range(2) for t in range(4)]
        part_words(1, slice(0, 1))
        part_words(1, slice(1, 2))
        round_wv(0, 0, nc.vector.tensor_copy, 0, 2, AT_WV00_ROUNDED)
        for b, half, t in gates[:8]:
            gate_tile(b, half, t)
        round_wv(0, 0, nc.vector.tensor_copy, 2, 2, AT_WV00_ROUNDED + 2 * KIB)
        load_wo(0)
        permute_wg(1)
        quantise_wv(0, 0, 0, 2)
        quantise_wv(0, 0, 2, 2)
        round_wv(0, 1, nc.vector.tensor_copy, 0, 2, AT_ROUNDED)
        round_wv(0, 1, nc.vector.tensor_copy, 2, 2, AT_ROUNDED + 2 * KIB)
        load_wo(1)
        quantise_wv(0, 1, 0, 2)
        quantise_wv(0, 1, 2, 2)
        for b, half, t in gates[8:EARLY_GATES]:
            gate_tile(b, half, t)
        round_wv(1, 0, nc.vector.tensor_copy, 0, 2, AT_ROUNDED)
        round_wv(1, 0, nc.scalar.copy, 2, 2)
        round_wv(1, 1, nc.scalar.copy, 0, 4)
        bo_cols = placed("bo_cols", [P, 4], F32, AT_TABLE)
        with nc.allow_non_contiguous_dma(reason="one value a partition"):
            nc.sync.dma_start(bo_cols[:], bo.rearrange("(nt p) -> p nt", p=P))
        round_wo(0, 0, N)
        round_wo(1, 0, N // 2)
        round_wo(1, N // 2, N // 2)

        for chunk in range(CHUNKS):
            value_chunk(0, chunk)
            if chunk == 0:
                quantise_wv(1, 0, 0, 2)
            if chunk == 2:
                quantise_wv(1, 0, 2, 2)
            if chunk == 4:
                quantise_h(0, 0, 4)
            if chunk == 5:
                quantise_wv(1, 1, 0, 4)
            if chunk == 7:
                quantise_wo(0, 0, N)
        for b, half, t in gates[EARLY_GATES:]:
            gate_tile(b, half, t)

        for chunk in range(4):
            value_chunk(1, chunk)
        quantise_wo(1, 0, N // 2)
        quantise_h(1, 0, 4)
        quantise_wo(1, N // 2, N // 2)
        value_chunk(1, 4)
        value_chunk(1, 5)
        for nt in range(4):
            out_bank(0, HALF, nt, 1, 4 + nt)
        quantise_h(0, 4, 4)
        value_chunk(1, 6)
        quantise_h(1, 4, 2)
        value_chunk(1, 7)
        out_bank(HALF, QUARTER, 0, 2, 4)
        out_bank(HALF, QUARTER, 2, 2, 5)
        quantise_h(1, 6, 1)
        quantise_h(1, 7, 1)
        last_piece((0, 1, 6, 2))
